import numpy as np
import ml_dtypes


def mxq(x, axis, fmt="e4m3"):
    dtype, down = {"e4m3": (ml_dtypes.float8_e4m3fn, 7), "e5m2": (ml_dtypes.float8_e5m2, 14)}[fmt]
    v = np.moveaxis(np.asarray(x, np.float32).astype(ml_dtypes.bfloat16).astype(np.float64), axis, -1)
    blocks = v.reshape(v.shape[:-1] + (-1, 32))
    amax = np.abs(blocks).max(-1, keepdims=True)
    byte = np.maximum(np.where(amax > 0, np.frexp(amax)[1] - 1 + 127, 0) - down, 1)
    scale = np.exp2(byte - 127.0)
    codes = (blocks / scale).astype(np.float32).astype(dtype).astype(np.float64)
    return np.moveaxis((codes * scale).reshape(v.shape), -1, axis)


WIDE = False


def mx_kscale(k):
    if not WIDE:
        return np.ones(k)
    levels = np.array([10, -10, 5, -5, 0])
    if k % 512:
        return np.exp2(np.random.permutation(np.resize(levels, k // 32))).repeat(32)
    a = np.empty((k // 512, 16))
    for p in range(k // 512):
        a[p, :8] = np.random.permutation(np.resize(levels, 8))
        for g in range(8):
            far = levels[np.abs(levels - a[p, g]) >= 10]
            a[p, g + 8] = far[np.random.randint(len(far))]
    return np.exp2(a.ravel()).repeat(32)


def f64(x):
    return np.asarray(x).astype(np.float64)


def striped(idx):
    return np.tile(idx.reshape(-1, 16).T, (8, 1)).astype(np.uint16)


def unstriped(offs):
    return offs[:16].T.reshape(-1).astype(np.int64)

def planes(y):
    n, m = y.shape
    v = y.astype(np.float32).astype(ml_dtypes.bfloat16).astype(np.float64).reshape(n // 32, 32, m)
    top = np.abs(v).max(1)
    byte = np.clip(np.where(top > 0, np.frexp(top)[1] - 1 + 127 - 7, 1), 1, 254)
    codes = (v * np.exp2(127.0 - byte)[:, None, :]).reshape(n, m).astype(np.float32).astype(ml_dtypes.float8_e4m3fn).view(np.uint8)
    words = codes.reshape(n // 512, 128, 4, m).transpose(0, 1, 3, 2)
    return np.ascontiguousarray(words), np.ascontiguousarray(byte.astype(np.uint8).reshape(n // 512, 16, m))


K, T, S, V, H = 512, 1024, 768, 256, 512


def setup_inputs():
    n = np.random.standard_normal
    s = mx_kscale(K)[:, None]
    u = mx_kscale(H)
    return {
        "xT": (n((K, T)) * s).astype(np.float32),
        "w1": (n((K, H)) / np.sqrt(K) / s * u).astype(np.float32),
        "w2": (n((K, H)) / np.sqrt(K) / s).astype(np.float32),
        "w3": (n((K, H)) / np.sqrt(K) / s).astype(np.float32),
        "w4": (n((H, H)) / np.sqrt(H) / u[:, None]).astype(np.float32),
        "offs": striped(np.random.permutation(T)[:S]),
    }


def reference(xT, w1, w2, w3, w4, offs):
    xq = mxq(f64(xT)[:, unstriped(offs)], 0, "e4m3")
    z = (((mxq(f64(w1), 0, "e4m3").T @ xq[:, :V])) * ((mxq(f64(w2), 0, "e4m3").T @ xq[:, V:2 * V]))) * ((mxq(f64(w3), 0, "e4m3").T @ xq[:, 2 * V:3 * V]))
    out_0 = mxq(f64(w4), 0, "e4m3").T @ mxq(z, 0, "e4m3")
    return (out_0,) + planes(out_0)

@@ -1,0 +1,193 @@
+from contextlib import ExitStack
+
+import concourse.mybir as mybir
+
+K, T, S, V, H = 512, 1024, 768, 256, 512
+FLOPS = 2 * 4 * K * H * V
+
+F32 = mybir.dt.float32
+BF16 = mybir.dt.bfloat16
+U32 = mybir.dt.uint32
+I32 = mybir.dt.int32
+U16 = mybir.dt.uint16
+U8 = mybir.dt.uint8
+FP8X4 = mybir.dt.float8_e4m3fn_x4
+MULT = mybir.AluOpType.mult
+
+P = 128
+PACK = 4
+HALF = V // 2
+ALIGN = 64
+CUT = 512
+SHARE = 864
+
+
+def tile_picked_trilin_none_lo_kernel(tc, xT, w1, w2, w3, w4, offs, out_0, out_1, out_2):
+    nc = tc.nc
+
+    def copy_on(engine, out, in_):
+        if engine == "vector":
+            nc.vector.tensor_copy(out=out, in_=in_)
+        else:
+            nc.scalar.copy(out=out, in_=in_)
+
+    with ExitStack() as ctx:
+        sb = ctx.enter_context(tc.tile_pool(name="sb", bufs=1))
+        ps = ctx.enter_context(tc.psum_pool(name="ps", bufs=1))
+
+        x_rows = xT.rearrange("(p j) c -> p j c", j=PACK)
+        offsets = sb.tile([P, S // 16], U16, name="offsets")
+        x_raw = [[None, None], [None, None]]
+        for a in range(2):
+            for c, (c0, c1) in enumerate(((0, CUT), (CUT, T))):
+                part = sb.tile([P, 2, c1 - c0], F32, name="x_raw%d_%d" % (a, c))
+                nc.sync.dma_start(out=part[:], in_=x_rows[:, 2 * a:2 * a + 2, c0:c1])
+                x_raw[a][c] = part
+            if a == 0:
+                nc.sync.dma_start(offsets[:], offs)
+        w_raw = []
+        for d, w in enumerate((w1, w2, w3, w4)):
+            raw = sb.tile([P, PACK, H], F32, name="w_raw%d" % d, tag="w_raw%d" % d, align_bytes=ALIGN)
+            nc.sync.dma_start(out=raw[:], in_=w.rearrange("(p j) c -> p j c", j=PACK))
+            w_raw.append(raw)
+
+        pairs = [sb.tile([P, 2 * T], BF16, name="pairs%d" % a, tag="pairs%d" % a, align_bytes=ALIGN) for a in range(2)]
+
+        def pair_up(engine, a, src, c0, c1, base):
+            copy_on(engine, pairs[a][:, 2 * c0:2 * c1].rearrange("p (c e) -> p c e", e=2), src[:, :, c0 - base:c1 - base].rearrange("p e c -> p c e"))
+
+        picked = [sb.tile([P, 2, V], U32, name="picked%d" % d, tag="picked%d" % d, align_bytes=ALIGN) for d in range(3)]
+
+        def gather(a, d):
+            window = pairs[a][:].bitcast(U32)
+            nc.vector.tensor_copy(out=picked[d][:, a, :], in_=window.indirect(offsets[:, 16 * d:16 * (d + 1)]))
+
+        woven = [sb.tile([P, V, 2], U32, name="woven%d" % d, align_bytes=ALIGN) for d in range(3)]
+
+        def weave(engine, d):
+            src = picked[d][:]
+            if engine == "vector":
+                nc.vector.tensor_copy(out=woven[d][:].bitcast(I32), in_=src.bitcast(I32).rearrange("p a c -> p c a"))
+            else:
+                nc.scalar.copy(out=woven[d][:], in_=src.rearrange("p a c -> p c a"))
+
+        x_codes = [sb.tile([P, V], U32, name="x_codes%d" % d, align_bytes=ALIGN) for d in range(3)]
+        x_scales = [sb.tile([P, V], U8, name="x_scales%d" % d, align_bytes=ALIGN) for d in range(3)]
+
+        def quantize_x(d):
+            nc.vector.quantize_mx(out=x_codes[d][:].bitcast(FP8X4), scales=x_scales[d][:],
+                                  in_=woven[d][:].rearrange("p c a -> p (c a)").bitcast(BF16))
+
+        w_bf = [[None, None] for d in range(4)]
+        w_codes = [[sb.tile([P, 2 * P], U32, name="w_codes%d_%d" % (d, u), align_bytes=ALIGN) for u in range(2)] for d in range(4)]
+        w_scales = [[sb.tile([P, 2 * P], U8, name="w_scales%d_%d" % (d, u), align_bytes=ALIGN) for u in range(2)] for d in range(4)]
+
+        def round_w(engine, d, u):
+            w_bf[d][u] = sb.tile([P, 2, P, PACK], BF16, name="w_bf%d_%d" % (d, u), align_bytes=ALIGN)
+            src = w_raw[d][:].rearrange("p j (m t) -> p m j t", t=PACK)[:, :, :, 2 * u:2 * u + 2]
+            copy_on(engine, w_bf[d][u][:].rearrange("p t m j -> p m j t"), src)
+
+        def quantize_w(d, u):
+            nc.vector.quantize_mx(out=w_codes[d][u][:].bitcast(FP8X4), scales=w_scales[d][u][:],
+                                  in_=w_bf[d][u][:].rearrange("p t m j -> p (t m j)"))
+
+        banks = [[ps.tile([P, PACK, HALF], F32, name="bank%d_%d" % (d, h)) for h in range(2)] for d in range(4)]
+
+        def multiply(d, u, h, codes, scales):
+            cols = slice(h * HALF, (h + 1) * HALF)
+            for e in range(2):
+                m = slice(e * P, (e + 1) * P)
+                nc.tensor.matmul_mx(out=banks[d][h][:, 2 * u + e, :],
+                                    lhsT=w_codes[d][u][:, m].bitcast(FP8X4), lhsT_scale=w_scales[d][u][:, m],
+                                    rhs=codes[:, cols].bitcast(FP8X4), rhs_scale=scales[:, cols],
+                                    start=True, stop=True)
+
+        def first_layer(d, order):
+            for u in order:
+                for h in range(2):
+                    multiply(d, u, h, x_codes[d], x_scales[d])
+
+        def woven_bank(d, h):
+            return banks[d][h][:].rearrange("p t v -> p v t")
+
+        y12 = [sb.tile([P, HALF, PACK], F32, name="y12_%d" % h) for h in range(2)]
+        z_bf = [sb.tile([P, HALF, PACK], BF16, name="z_bf%d" % h, align_bytes=ALIGN) for h in range(2)]
+        z_codes = sb.tile([P, V], U32, name="z_codes", align_bytes=ALIGN)
+        z_scales = sb.tile([P, V], U8, name="z_scales", align_bytes=ALIGN)
+
+        result = [sb.tile([P, PACK, HALF], F32, name="result%d" % h) for h in range(2)]
+        r_bf = [sb.tile([P, HALF, PACK], BF16, name="r_bf%d" % h, align_bytes=ALIGN) for h in range(2)]
+        r_codes = sb.tile([P, V], U32, name="r_codes", align_bytes=ALIGN)
+        r_scales = sb.tile([P, V], U8, name="r_scales", align_bytes=ALIGN)
+        out_rows = out_0.rearrange("(p t) v -> p t v", t=PACK)
+
+        def last_factor(h):
+            nc.vector.tensor_tensor(out=z_bf[h][:], in0=woven_bank(2, h), in1=y12[h][:], op=MULT)
+
+        def quantize_half(h, codes, scales, values):
+            cols = slice(h * HALF, (h + 1) * HALF)
+            nc.vector.quantize_mx(out=codes[:, cols].bitcast(FP8X4), scales=scales[:, cols],
+                                  in_=values[h][:].rearrange("p v t -> p (v t)"))
+
+        def store_half(engine, h):
+            copy_on(engine, result[h][:], banks[3][h][:])
+            nc.sync.dma_start(out=out_rows[:, :, h * HALF:(h + 1) * HALF], in_=result[h][:])
+
+        pair_up("vector", 0, x_raw[0][0], 0, CUT, 0)
+        pair_up("vector", 0, x_raw[0][1], CUT, SHARE, CUT)
+        pair_up("scalar", 0, x_raw[0][1], SHARE, T, CUT)
+        for d in range(3):
+            gather(0, d)
+        pair_up("scalar", 1, x_raw[1][0], 0, CUT, 0)
+        pair_up("scalar", 1, x_raw[1][1], SHARE, T, CUT)
+        pair_up("vector", 1, x_raw[1][1], CUT, SHARE, CUT)
+        for d in range(3):
+            gather(1, d)
+        weave("scalar", 0)
+        weave("vector", 1)
+        weave("vector", 2)
+        round_w("scalar", 0, 0)
+        round_w("scalar", 0, 1)
+        for d in range(3):
+            quantize_x(d)
+        quantize_w(0, 0)
+        round_w("vector", 1, 1)
+        quantize_w(0, 1)
+        first_layer(0, (0, 1))
+        round_w("scalar", 1, 0)
+        quantize_w(1, 1)
+        quantize_w(1, 0)
+        round_w("vector", 2, 1)
+        first_layer(1, (1, 0))
+        round_w("scalar", 2, 0)
+        quantize_w(2, 1)
+        quantize_w(2, 0)
+        first_layer(2, (1, 0))
+        y1 = sb.tile([P, 2, HALF, PACK], F32, name="y1", tag="w_raw2", align_bytes=ALIGN)
+        for h in range(2):
+            nc.scalar.copy(out=y1[:, h, :, :], in_=woven_bank(0, h))
+        for h in range(2):
+            nc.vector.tensor_tensor(out=y12[h][:], in0=woven_bank(1, h), in1=y1[:, h, :, :], op=MULT)
+        round_w("scalar", 3, 0)
+        round_w("scalar", 3, 1)
+        last_factor(0)
+        last_factor(1)
+        quantize_w(3, 0)
+        quantize_half(0, z_codes, z_scales, z_bf)
+        quantize_half(1, z_codes, z_scales, z_bf)
+        quantize_w(3, 1)
+        for u in range(2):
+            for h in range(2):
+                multiply(3, u, h, z_codes, z_scales)
+
+        nc.vector.tensor_copy(out=r_bf[0][:], in_=woven_bank(3, 0))
+        nc.scalar.copy(out=r_bf[1][:], in_=woven_bank(3, 1))
+        store_half("scalar", 0)
+        for h in range(2):
+            quantize_half(h, r_codes, r_scales, r_bf)
+        store_half("vector", 1)
+        words = out_1.rearrange("z p c r -> (z p) (c r)").bitcast(I32)
+        nc.sync.dma_start(out=words, in_=r_codes[:].bitcast(I32))
+        rows = out_2.rearrange("z q c -> (z q) c").bitcast(I32)
+        for q in range(4):
+            nc.sync.dma_start(out=rows[4 * q:4 * q + 4, :], in_=r_scales[32 * q:32 * q + 4, :].bitcast(I32))

@@ -19,7 +19,8 @@ PACK = 4
 HALF = V // 2
 ALIGN = 64
 CUT = 512
-SHARE = 864
+SHARE = 768
+LOW_SHARE = 704
 
 
 def tile_picked_trilin_none_lo_kernel(tc, xT, w1, w2, w3, w4, offs, out_0, out_1, out_2):
@@ -36,15 +37,15 @@ def tile_picked_trilin_none_lo_kernel(tc, xT, w1, w2, w3, w4, offs, out_0, out_1
         ps = ctx.enter_context(tc.psum_pool(name="ps", bufs=1))
 
         x_rows = xT.rearrange("(p j) c -> p j c", j=PACK)
+        x_low = sb.tile([P, 2, T], F32, name="x_low")
+        nc.sync.dma_start(out=x_low[:], in_=x_rows[:, 0:2, :])
         offsets = sb.tile([P, S // 16], U16, name="offsets")
-        x_raw = [[None, None], [None, None]]
-        for a in range(2):
-            for c, (c0, c1) in enumerate(((0, CUT), (CUT, T))):
-                part = sb.tile([P, 2, c1 - c0], F32, name="x_raw%d_%d" % (a, c))
-                nc.sync.dma_start(out=part[:], in_=x_rows[:, 2 * a:2 * a + 2, c0:c1])
-                x_raw[a][c] = part
-            if a == 0:
-                nc.sync.dma_start(offsets[:], offs)
+        nc.sync.dma_start(offsets[:], offs)
+        x_high = []
+        for c in range(2):
+            part = sb.tile([P, 2, CUT], F32, name="x_high%d" % c)
+            nc.sync.dma_start(out=part[:], in_=x_rows[:, 2:4, c * CUT:(c + 1) * CUT])
+            x_high.append(part)
         w_raw = []
         for d, w in enumerate((w1, w2, w3, w4)):
             raw = sb.tile([P, PACK, H], F32, name="w_raw%d" % d, tag="w_raw%d" % d, align_bytes=ALIGN)
@@ -115,7 +116,7 @@ def tile_picked_trilin_none_lo_kernel(tc, xT, w1, w2, w3, w4, offs, out_0, out_1
         z_codes = sb.tile([P, V], U32, name="z_codes", align_bytes=ALIGN)
         z_scales = sb.tile([P, V], U8, name="z_scales", align_bytes=ALIGN)
 
-        result = [sb.tile([P, PACK, HALF], F32, name="result%d" % h) for h in range(2)]
+        result = sb.tile([P, PACK, V], F32, name="result")
         r_bf = [sb.tile([P, HALF, PACK], BF16, name="r_bf%d" % h, align_bytes=ALIGN) for h in range(2)]
         r_codes = sb.tile([P, V], U32, name="r_codes", align_bytes=ALIGN)
         r_scales = sb.tile([P, V], U8, name="r_scales", align_bytes=ALIGN)
@@ -129,18 +130,13 @@ def tile_picked_trilin_none_lo_kernel(tc, xT, w1, w2, w3, w4, offs, out_0, out_1
             nc.vector.quantize_mx(out=codes[:, cols].bitcast(FP8X4), scales=scales[:, cols],
                                   in_=values[h][:].rearrange("p v t -> p (v t)"))
 
-        def store_half(engine, h):
-            copy_on(engine, result[h][:], banks[3][h][:])
-            nc.sync.dma_start(out=out_rows[:, :, h * HALF:(h + 1) * HALF], in_=result[h][:])
-
-        pair_up("vector", 0, x_raw[0][0], 0, CUT, 0)
-        pair_up("vector", 0, x_raw[0][1], CUT, SHARE, CUT)
-        pair_up("scalar", 0, x_raw[0][1], SHARE, T, CUT)
+        pair_up("vector", 0, x_low, 0, LOW_SHARE, 0)
+        pair_up("scalar", 0, x_low, LOW_SHARE, T, 0)
         for d in range(3):
             gather(0, d)
-        pair_up("scalar", 1, x_raw[1][0], 0, CUT, 0)
-        pair_up("scalar", 1, x_raw[1][1], SHARE, T, CUT)
-        pair_up("vector", 1, x_raw[1][1], CUT, SHARE, CUT)
+        pair_up("scalar", 1, x_high[0], 0, CUT, 0)
+        pair_up("scalar", 1, x_high[1], SHARE, T, CUT)
+        pair_up("vector", 1, x_high[1], CUT, SHARE, CUT)
         for d in range(3):
             gather(1, d)
         weave("scalar", 0)
@@ -180,14 +176,16 @@ def tile_picked_trilin_none_lo_kernel(tc, xT, w1, w2, w3, w4, offs, out_0, out_1
             for h in range(2):
                 multiply(3, u, h, z_codes, z_scales)
 
-        nc.vector.tensor_copy(out=r_bf[0][:], in_=woven_bank(3, 0))
+        nc.scalar.copy(out=result[:, :, 0:HALF], in_=banks[3][0][:])
+        nc.vector.tensor_copy(out=result[:, :, HALF:V], in_=banks[3][1][:])
+        nc.sync.dma_start(out=out_rows, in_=result[:])
+        nc.vector.tensor_copy(out=r_bf[0][:], in_=result[:, :, 0:HALF].rearrange("p t v -> p v t"))
         nc.scalar.copy(out=r_bf[1][:], in_=woven_bank(3, 1))
-        store_half("scalar", 0)
         for h in range(2):
             quantize_half(h, r_codes, r_scales, r_bf)
-        store_half("vector", 1)
         words = out_1.rearrange("z p c r -> (z p) (c r)").bitcast(I32)
         nc.sync.dma_start(out=words, in_=r_codes[:].bitcast(I32))
         rows = out_2.rearrange("z q c -> (z q) c").bitcast(I32)
         for q in range(4):
-            nc.sync.dma_start(out=rows[4 * q:4 * q + 4, :], in_=r_scales[32 * q:32 * q + 4, :].bitcast(I32))
+            queue = nc.scalar if q < 3 else nc.sync
+            queue.dma_start(out=rows[4 * q:4 * q + 4, :], in_=r_scales[32 * q:32 * q + 4, :].bitcast(I32))

@@ -18,8 +18,7 @@ P = 128
 PACK = 4
 HALF = V // 2
 ALIGN = 64
-CUT = 512
-SHARE = 768
+HIGH_SHARE = 416
 LOW_SHARE = 704
 
 
@@ -41,11 +40,8 @@ def tile_picked_trilin_none_lo_kernel(tc, xT, w1, w2, w3, w4, offs, out_0, out_1
         nc.sync.dma_start(out=x_low[:], in_=x_rows[:, 0:2, :])
         offsets = sb.tile([P, S // 16], U16, name="offsets")
         nc.sync.dma_start(offsets[:], offs)
-        x_high = []
-        for c in range(2):
-            part = sb.tile([P, 2, CUT], F32, name="x_high%d" % c)
-            nc.sync.dma_start(out=part[:], in_=x_rows[:, 2:4, c * CUT:(c + 1) * CUT])
-            x_high.append(part)
+        x_high = sb.tile([P, 2, T], F32, name="x_high")
+        nc.sync.dma_start(out=x_high[:], in_=x_rows[:, 2:4, :])
         w_raw = []
         for d, w in enumerate((w1, w2, w3, w4)):
             raw = sb.tile([P, PACK, H], F32, name="w_raw%d" % d, tag="w_raw%d" % d, align_bytes=ALIGN)
@@ -134,9 +130,8 @@ def tile_picked_trilin_none_lo_kernel(tc, xT, w1, w2, w3, w4, offs, out_0, out_1
         pair_up("scalar", 0, x_low, LOW_SHARE, T, 0)
         for d in range(3):
             gather(0, d)
-        pair_up("scalar", 1, x_high[0], 0, CUT, 0)
-        pair_up("scalar", 1, x_high[1], SHARE, T, CUT)
-        pair_up("vector", 1, x_high[1], CUT, SHARE, CUT)
+        pair_up("scalar", 1, x_high, HIGH_SHARE, T, 0)
+        pair_up("vector", 1, x_high, 0, HIGH_SHARE, 0)
         for d in range(3):
             gather(1, d)
         weave("scalar", 0)

@@ -18,8 +18,8 @@ P = 128
 PACK = 4
 HALF = V // 2
 ALIGN = 64
-HIGH_SHARE = 416
-LOW_SHARE = 704
+LOW_CUTS = (0, 768, T)
+HIGH_CUTS = (0, 384, 768, T)
 
 
 def tile_picked_trilin_none_lo_kernel(tc, xT, w1, w2, w3, w4, offs, out_0, out_1, out_2):
@@ -36,12 +36,15 @@ def tile_picked_trilin_none_lo_kernel(tc, xT, w1, w2, w3, w4, offs, out_0, out_1
         ps = ctx.enter_context(tc.psum_pool(name="ps", bufs=1))
 
         x_rows = xT.rearrange("(p j) c -> p j c", j=PACK)
-        x_low = sb.tile([P, 2, T], F32, name="x_low")
-        nc.sync.dma_start(out=x_low[:], in_=x_rows[:, 0:2, :])
         offsets = sb.tile([P, S // 16], U16, name="offsets")
-        nc.sync.dma_start(offsets[:], offs)
-        x_high = sb.tile([P, 2, T], F32, name="x_high")
-        nc.sync.dma_start(out=x_high[:], in_=x_rows[:, 2:4, :])
+        x_raw = [[], []]
+        for a, cuts in enumerate((LOW_CUTS, HIGH_CUTS)):
+            for c0, c1 in zip(cuts, cuts[1:]):
+                part = sb.tile([P, 2, c1 - c0], F32, name="x_raw%d_%d" % (a, c0))
+                nc.sync.dma_start(out=part[:], in_=x_rows[:, 2 * a:2 * a + 2, c0:c1])
+                x_raw[a].append(part)
+            if a == 0:
+                nc.sync.dma_start(offsets[:], offs)
         w_raw = []
         for d, w in enumerate((w1, w2, w3, w4)):
             raw = sb.tile([P, PACK, H], F32, name="w_raw%d" % d, tag="w_raw%d" % d, align_bytes=ALIGN)
@@ -107,7 +110,6 @@ def tile_picked_trilin_none_lo_kernel(tc, xT, w1, w2, w3, w4, offs, out_0, out_1
         def woven_bank(d, h):
             return banks[d][h][:].rearrange("p t v -> p v t")
 
-        y12 = [sb.tile([P, HALF, PACK], F32, name="y12_%d" % h) for h in range(2)]
         z_bf = [sb.tile([P, HALF, PACK], BF16, name="z_bf%d" % h, align_bytes=ALIGN) for h in range(2)]
         z_codes = sb.tile([P, V], U32, name="z_codes", align_bytes=ALIGN)
         z_scales = sb.tile([P, V], U8, name="z_scales", align_bytes=ALIGN)
@@ -118,20 +120,23 @@ def tile_picked_trilin_none_lo_kernel(tc, xT, w1, w2, w3, w4, offs, out_0, out_1
         r_scales = sb.tile([P, V], U8, name="r_scales", align_bytes=ALIGN)
         out_rows = out_0.rearrange("(p t) v -> p t v", t=PACK)
 
-        def last_factor(h):
-            nc.vector.tensor_tensor(out=z_bf[h][:], in0=woven_bank(2, h), in1=y12[h][:], op=MULT)
+        def last_factor(h, y12):
+            nc.vector.tensor_tensor(out=z_bf[h][:], in0=woven_bank(2, h), in1=y12[h], op=MULT)
 
         def quantize_half(h, codes, scales, values):
             cols = slice(h * HALF, (h + 1) * HALF)
             nc.vector.quantize_mx(out=codes[:, cols].bitcast(FP8X4), scales=scales[:, cols],
                                   in_=values[h][:].rearrange("p v t -> p (v t)"))
 
-        pair_up("vector", 0, x_low, 0, LOW_SHARE, 0)
-        pair_up("scalar", 0, x_low, LOW_SHARE, T, 0)
+        pair_up("vector", 0, x_raw[0][0], 0, 512, 0)
+        pair_up("scalar", 0, x_raw[0][0], 512, 768, 0)
+        pair_up("vector", 0, x_raw[0][1], 768, 960, 768)
+        pair_up("scalar", 0, x_raw[0][1], 960, T, 768)
         for d in range(3):
             gather(0, d)
-        pair_up("scalar", 1, x_high, HIGH_SHARE, T, 0)
-        pair_up("vector", 1, x_high, 0, HIGH_SHARE, 0)
+        pair_up("scalar", 1, x_raw[1][0], 0, 384, 0)
+        pair_up("scalar", 1, x_raw[1][1], 384, 768, 384)
+        pair_up("vector", 1, x_raw[1][2], 768, T, 768)
         for d in range(3):
             gather(1, d)
         weave("scalar", 0)
@@ -148,21 +153,25 @@ def tile_picked_trilin_none_lo_kernel(tc, xT, w1, w2, w3, w4, offs, out_0, out_1
         round_w("scalar", 1, 0)
         quantize_w(1, 1)
         quantize_w(1, 0)
+        y1_first = sb.tile([P, HALF, PACK], F32, name="y1_first", tag="w_raw1", align_bytes=ALIGN)
+        nc.scalar.copy(out=y1_first[:], in_=woven_bank(0, 0))
         round_w("vector", 2, 1)
         first_layer(1, (1, 0))
         round_w("scalar", 2, 0)
         quantize_w(2, 1)
         quantize_w(2, 0)
         first_layer(2, (1, 0))
-        y1 = sb.tile([P, 2, HALF, PACK], F32, name="y1", tag="w_raw2", align_bytes=ALIGN)
+        late = sb.tile([P, 2, HALF, PACK], F32, name="late", tag="w_raw2", align_bytes=ALIGN)
+        y12_second = sb.tile([P, HALF, PACK], F32, name="y12_second")
+        y1 = [y1_first[:], late[:, 0, :, :]]
+        y12 = [late[:, 1, :, :], y12_second[:]]
+        nc.scalar.copy(out=y1[1], in_=woven_bank(0, 1))
         for h in range(2):
-            nc.scalar.copy(out=y1[:, h, :, :], in_=woven_bank(0, h))
-        for h in range(2):
-            nc.vector.tensor_tensor(out=y12[h][:], in0=woven_bank(1, h), in1=y1[:, h, :, :], op=MULT)
+            nc.vector.tensor_tensor(out=y12[h], in0=woven_bank(1, h), in1=y1[h], op=MULT)
         round_w("scalar", 3, 0)
         round_w("scalar", 3, 1)
-        last_factor(0)
-        last_factor(1)
+        last_factor(0, y12)
+        last_factor(1, y12)
         quantize_w(3, 0)
         quantize_half(0, z_codes, z_scales, z_bf)
         quantize_half(1, z_codes, z_scales, z_bf)

@@ -18,8 +18,7 @@ P = 128
 PACK = 4
 HALF = V // 2
 ALIGN = 64
-LOW_CUTS = (0, 768, T)
-HIGH_CUTS = (0, 384, 768, T)
+COPY = mybir.ActivationFunctionType.Copy
 
 
 def tile_picked_trilin_none_lo_kernel(tc, xT, w1, w2, w3, w4, offs, out_0, out_1, out_2):
@@ -37,46 +36,46 @@ def tile_picked_trilin_none_lo_kernel(tc, xT, w1, w2, w3, w4, offs, out_0, out_1
 
         x_rows = xT.rearrange("(p j) c -> p j c", j=PACK)
         offsets = sb.tile([P, S // 16], U16, name="offsets")
-        x_raw = [[], []]
-        for a, cuts in enumerate((LOW_CUTS, HIGH_CUTS)):
-            for c0, c1 in zip(cuts, cuts[1:]):
-                part = sb.tile([P, 2, c1 - c0], F32, name="x_raw%d_%d" % (a, c0))
-                nc.sync.dma_start(out=part[:], in_=x_rows[:, 2 * a:2 * a + 2, c0:c1])
-                x_raw[a].append(part)
-            if a == 0:
+        planes = []
+        for j in range(PACK):
+            plane = sb.tile([P, T], F32, name="plane%d" % j, align_bytes=ALIGN)
+            nc.sync.dma_start(out=plane[:], in_=x_rows[:, j, :])
+            planes.append(plane)
+            if j == 0:
                 nc.sync.dma_start(offsets[:], offs)
         w_raw = []
         for d, w in enumerate((w1, w2, w3, w4)):
             raw = sb.tile([P, PACK, H], F32, name="w_raw%d" % d, tag="w_raw%d" % d, align_bytes=ALIGN)
-            nc.sync.dma_start(out=raw[:], in_=w.rearrange("(p j) c -> p j c", j=PACK))
+            nc.sync.dma_start(out=raw[:].rearrange("p j c -> p (j c)"), in_=w.rearrange("(p j) c -> p (j c)", j=PACK))
             w_raw.append(raw)
 
-        pairs = [sb.tile([P, 2 * T], BF16, name="pairs%d" % a, tag="pairs%d" % a, align_bytes=ALIGN) for a in range(2)]
+        picked_two = sb.tile([P, PACK, 2 * V], BF16, name="picked_two", align_bytes=ALIGN)
+        picked_last = sb.tile([P, PACK, V], BF16, name="picked_last", align_bytes=ALIGN)
 
-        def pair_up(engine, a, src, c0, c1, base):
-            copy_on(engine, pairs[a][:, 2 * c0:2 * c1].rearrange("p (c e) -> p c e", e=2), src[:, :, c0 - base:c1 - base].rearrange("p e c -> p c e"))
+        def gather(engine, j, d0, d1):
+            out = picked_two[:, j, d0 * V:d1 * V] if d0 < 2 else picked_last[:, j, :]
+            looked_up = planes[j][:].indirect(offsets[:, 16 * d0:16 * d1])
+            if engine == "vector":
+                nc.vector.tensor_copy(out=out, in_=looked_up)
+            else:
+                nc.scalar.activation(out, looked_up, COPY)
 
-        picked = [sb.tile([P, 2, V], U32, name="picked%d" % d, tag="picked%d" % d, align_bytes=ALIGN) for d in range(3)]
-
-        def gather(a, d):
-            window = pairs[a][:].bitcast(U32)
-            nc.vector.tensor_copy(out=picked[d][:, a, :], in_=window.indirect(offsets[:, 16 * d:16 * (d + 1)]))
-
-        woven = [sb.tile([P, V, 2], U32, name="woven%d" % d, align_bytes=ALIGN) for d in range(3)]
+        woven_two = sb.tile([P, 2 * V, PACK], BF16, name="woven_two", align_bytes=ALIGN)
+        woven_last = sb.tile([P, V, PACK], BF16, name="woven_last", align_bytes=ALIGN)
 
         def weave(engine, d):
-            src = picked[d][:]
-            if engine == "vector":
-                nc.vector.tensor_copy(out=woven[d][:].bitcast(I32), in_=src.bitcast(I32).rearrange("p a c -> p c a"))
-            else:
-                nc.scalar.copy(out=woven[d][:], in_=src.rearrange("p a c -> p c a"))
+            src = picked_two[:, :, d * V:(d + 1) * V] if d < 2 else picked_last[:]
+            dst = woven_two[:, d * V:(d + 1) * V, :] if d < 2 else woven_last[:]
+            copy_on(engine, dst.rearrange("p (c i) j -> p c j i", i=4), src.rearrange("p j (c i) -> p c j i", i=4))
 
-        x_codes = [sb.tile([P, V], U32, name="x_codes%d" % d, align_bytes=ALIGN) for d in range(3)]
-        x_scales = [sb.tile([P, V], U8, name="x_scales%d" % d, align_bytes=ALIGN) for d in range(3)]
+        x_words = sb.tile([P, S], U32, name="x_words", align_bytes=ALIGN)
+        x_bytes = sb.tile([P, S], U8, name="x_bytes", align_bytes=ALIGN)
+        x_codes = [x_words[:, d * V:(d + 1) * V] for d in range(3)]
+        x_scales = [x_bytes[:, d * V:(d + 1) * V] for d in range(3)]
 
-        def quantize_x(d):
-            nc.vector.quantize_mx(out=x_codes[d][:].bitcast(FP8X4), scales=x_scales[d][:],
-                                  in_=woven[d][:].rearrange("p c a -> p (c a)").bitcast(BF16))
+        def quantize_x(values, e0, e1):
+            nc.vector.quantize_mx(out=x_words[:, e0:e1].bitcast(FP8X4), scales=x_bytes[:, e0:e1],
+                                  in_=values[:].rearrange("p c j -> p (c j)"))
 
         w_bf = [[None, None] for d in range(4)]
         w_codes = [[sb.tile([P, 2 * P], U32, name="w_codes%d_%d" % (d, u), align_bytes=ALIGN) for u in range(2)] for d in range(4)]
@@ -128,24 +127,21 @@ def tile_picked_trilin_none_lo_kernel(tc, xT, w1, w2, w3, w4, offs, out_0, out_1
             nc.vector.quantize_mx(out=codes[:, cols].bitcast(FP8X4), scales=scales[:, cols],
                                   in_=values[h][:].rearrange("p v t -> p (v t)"))
 
-        pair_up("vector", 0, x_raw[0][0], 0, 512, 0)
-        pair_up("scalar", 0, x_raw[0][0], 512, 768, 0)
-        pair_up("vector", 0, x_raw[0][1], 768, 960, 768)
-        pair_up("scalar", 0, x_raw[0][1], 960, T, 768)
+        idle = sb.tile([P, 2], F32, name="idle")
+        nc.gpsimd.memset(idle[:, 0:1], 0.0)
+        nc.scalar.copy(out=idle[:, 1:2], in_=idle[:, 0:1])
+
+        for j, engine in ((0, "vector"), (1, "scalar"), (2, "vector")):
+            gather(engine, j, 0, 2)
+            gather(engine, j, 2, 3)
         for d in range(3):
-            gather(0, d)
-        pair_up("scalar", 1, x_raw[1][0], 0, 384, 0)
-        pair_up("scalar", 1, x_raw[1][1], 384, 768, 384)
-        pair_up("vector", 1, x_raw[1][2], 768, T, 768)
+            gather("scalar", 3, d, d + 1)
         for d in range(3):
-            gather(1, d)
-        weave("scalar", 0)
-        weave("vector", 1)
-        weave("vector", 2)
+            weave("vector", d)
         round_w("scalar", 0, 0)
         round_w("scalar", 0, 1)
-        for d in range(3):
-            quantize_x(d)
+        quantize_x(woven_two, 0, 2 * V)
+        quantize_x(woven_last, 2 * V, S)
         quantize_w(0, 0)
         round_w("vector", 1, 1)
         quantize_w(0, 1)
@@ -183,8 +179,8 @@ def tile_picked_trilin_none_lo_kernel(tc, xT, w1, w2, w3, w4, offs, out_0, out_1
         nc.scalar.copy(out=result[:, :, 0:HALF], in_=banks[3][0][:])
         nc.vector.tensor_copy(out=result[:, :, HALF:V], in_=banks[3][1][:])
         nc.sync.dma_start(out=out_rows, in_=result[:])
-        nc.vector.tensor_copy(out=r_bf[0][:], in_=result[:, :, 0:HALF].rearrange("p t v -> p v t"))
-        nc.scalar.copy(out=r_bf[1][:], in_=woven_bank(3, 1))
+        nc.scalar.copy(out=r_bf[0][:], in_=woven_bank(3, 0))
+        nc.vector.tensor_copy(out=r_bf[1][:], in_=woven_bank(3, 1))
         for h in range(2):
             quantize_half(h, r_codes, r_scales, r_bf)
         words = out_1.rearrange("z p c r -> (z p) (c r)").bitcast(I32)

@@ -90,7 +90,12 @@ def tile_picked_trilin_none_lo_kernel(tc, xT, w1, w2, w3, w4, offs, out_0, out_1
             nc.vector.quantize_mx(out=w_codes[d][u][:].bitcast(FP8X4), scales=w_scales[d][u][:],
                                   in_=w_bf[d][u][:].rearrange("p t m j -> p (t m j)"))
 
-        banks = [[ps.tile([P, PACK, HALF], F32, name="bank%d_%d" % (d, h)) for h in range(2)] for d in range(4)]
+        banks = [[ps.tile([P, PACK, HALF], F32, name="bank%d_%d" % (d, h), tag="bank%d_%d" % (d, h)) for h in range(2)] for d in range(4)]
+
+        def warm_up(tag):
+            spare = ps.tile([P, 2 * V], F32, name="spare_" + tag, tag=tag)
+            nc.tensor.matmul_mx(out=spare[:], lhsT=w_codes[2][0][:, 0:P].bitcast(FP8X4), lhsT_scale=w_scales[2][0][:, 0:P],
+                                rhs=x_words[:, 0:2 * V].bitcast(FP8X4), rhs_scale=x_bytes[:, 0:2 * V], start=True, stop=True)
 
         def multiply(d, u, h, codes, scales):
             cols = slice(h * HALF, (h + 1) * HALF)
@@ -168,6 +173,8 @@ def tile_picked_trilin_none_lo_kernel(tc, xT, w1, w2, w3, w4, offs, out_0, out_1
         round_w("scalar", 3, 1)
         last_factor(0, y12)
         last_factor(1, y12)
+        warm_up("bank1_1")
+        warm_up("bank2_0")
         quantize_w(3, 0)
         quantize_half(0, z_codes, z_scales, z_bf)
         quantize_half(1, z_codes, z_scales, z_bf)

@@ -49,23 +49,22 @@ def tile_picked_trilin_none_lo_kernel(tc, xT, w1, w2, w3, w4, offs, out_0, out_1
             nc.sync.dma_start(out=raw[:].rearrange("p j c -> p (j c)"), in_=w.rearrange("(p j) c -> p (j c)", j=PACK))
             w_raw.append(raw)
 
-        picked_two = sb.tile([P, PACK, 2 * V], BF16, name="picked_two", align_bytes=ALIGN)
-        picked_last = sb.tile([P, PACK, V], BF16, name="picked_last", align_bytes=ALIGN)
+        picked_first = sb.tile([P, PACK, V], BF16, name="picked_first", align_bytes=ALIGN)
+        picked_rest = sb.tile([P, PACK, 2 * V], BF16, name="picked_rest", align_bytes=ALIGN)
 
         def gather(engine, j, d0, d1):
-            out = picked_two[:, j, d0 * V:d1 * V] if d0 < 2 else picked_last[:, j, :]
+            out = picked_first[:, j, :] if d0 == 0 else picked_rest[:, j, :]
             looked_up = planes[j][:].indirect(offsets[:, 16 * d0:16 * d1])
             if engine == "vector":
                 nc.vector.tensor_copy(out=out, in_=looked_up)
             else:
                 nc.scalar.activation(out, looked_up, COPY)
 
-        woven_two = sb.tile([P, 2 * V, PACK], BF16, name="woven_two", align_bytes=ALIGN)
-        woven_last = sb.tile([P, V, PACK], BF16, name="woven_last", align_bytes=ALIGN)
+        woven = [sb.tile([P, V, PACK], BF16, name="woven%d" % d, align_bytes=ALIGN) for d in range(3)]
 
         def weave(engine, d):
-            src = picked_two[:, :, d * V:(d + 1) * V] if d < 2 else picked_last[:]
-            dst = woven_two[:, d * V:(d + 1) * V, :] if d < 2 else woven_last[:]
+            src = picked_first[:] if d == 0 else picked_rest[:, :, (d - 1) * V:d * V]
+            dst = woven[d][:]
             copy_on(engine, dst.rearrange("p (c i) j -> p c j i", i=4), src.rearrange("p j (c i) -> p c j i", i=4))
 
         x_words = sb.tile([P, S], U32, name="x_words", align_bytes=ALIGN)
@@ -73,16 +72,16 @@ def tile_picked_trilin_none_lo_kernel(tc, xT, w1, w2, w3, w4, offs, out_0, out_1
         x_codes = [x_words[:, d * V:(d + 1) * V] for d in range(3)]
         x_scales = [x_bytes[:, d * V:(d + 1) * V] for d in range(3)]
 
-        def quantize_x(values, e0, e1):
-            nc.vector.quantize_mx(out=x_words[:, e0:e1].bitcast(FP8X4), scales=x_bytes[:, e0:e1],
-                                  in_=values[:].rearrange("p c j -> p (c j)"))
+        def quantize_x(d):
+            nc.vector.quantize_mx(out=x_codes[d].bitcast(FP8X4), scales=x_scales[d],
+                                  in_=woven[d][:].rearrange("p c j -> p (c j)"))
 
         w_bf = [[None, None] for d in range(4)]
         w_codes = [[sb.tile([P, 2 * P], U32, name="w_codes%d_%d" % (d, u), align_bytes=ALIGN) for u in range(2)] for d in range(4)]
         w_scales = [[sb.tile([P, 2 * P], U8, name="w_scales%d_%d" % (d, u), align_bytes=ALIGN) for u in range(2)] for d in range(4)]
 
         def round_w(engine, d, u):
-            w_bf[d][u] = sb.tile([P, 2, P, PACK], BF16, name="w_bf%d_%d" % (d, u), align_bytes=ALIGN)
+            w_bf[d][u] = sb.tile([P, 2, P, PACK], BF16, name="w_bf%d_%d" % (d, u), tag="w_bf%d_%d" % (d, u), align_bytes=ALIGN)
             src = w_raw[d][:].rearrange("p j (m t) -> p m j t", t=PACK)[:, :, :, 2 * u:2 * u + 2]
             copy_on(engine, w_bf[d][u][:].rearrange("p t m j -> p m j t"), src)
 
@@ -136,28 +135,31 @@ def tile_picked_trilin_none_lo_kernel(tc, xT, w1, w2, w3, w4, offs, out_0, out_1
         nc.gpsimd.memset(idle[:, 0:1], 0.0)
         nc.scalar.copy(out=idle[:, 1:2], in_=idle[:, 0:1])
 
-        for j, engine in ((0, "vector"), (1, "scalar"), (2, "vector")):
-            gather(engine, j, 0, 2)
-            gather(engine, j, 2, 3)
-        for d in range(3):
-            gather("scalar", 3, d, d + 1)
-        for d in range(3):
-            weave("vector", d)
+        gather("vector", 0, 0, 1)
+        gather("vector", 0, 1, 3)
+        gather("scalar", 1, 1, 3)
+        gather("vector", 1, 0, 1)
+        for j in (2, 3):
+            gather("scalar", j, 0, 1)
+            gather("vector", j, 1, 3)
+        weave("scalar", 0)
+        weave("vector", 1)
+        weave("vector", 2)
         round_w("scalar", 0, 0)
         round_w("scalar", 0, 1)
-        quantize_x(woven_two, 0, 2 * V)
-        quantize_x(woven_last, 2 * V, S)
+        for d in (1, 2, 0):
+            quantize_x(d)
         quantize_w(0, 0)
-        round_w("vector", 1, 1)
         quantize_w(0, 1)
+        round_w("vector", 1, 1)
         first_layer(0, (0, 1))
         round_w("scalar", 1, 0)
-        quantize_w(1, 1)
         quantize_w(1, 0)
+        quantize_w(1, 1)
         y1_first = sb.tile([P, HALF, PACK], F32, name="y1_first", tag="w_raw1", align_bytes=ALIGN)
         nc.scalar.copy(out=y1_first[:], in_=woven_bank(0, 0))
         round_w("vector", 2, 1)
-        first_layer(1, (1, 0))
+        first_layer(1, (0, 1))
         round_w("scalar", 2, 0)
         quantize_w(2, 1)
         quantize_w(2, 0)

@@ -13,12 +13,14 @@ U16 = mybir.dt.uint16
 U8 = mybir.dt.uint8
 FP8X4 = mybir.dt.float8_e4m3fn_x4
 MULT = mybir.AluOpType.mult
+ADD = mybir.AluOpType.add
 
 P = 128
 PACK = 4
 HALF = V // 2
 ALIGN = 64
 COPY = mybir.ActivationFunctionType.Copy
+CUTS = ((0, 128), (0, 128), (0, 128), (0, 128))
 
 
 def tile_picked_trilin_none_lo_kernel(tc, xT, w1, w2, w3, w4, offs, out_0, out_1, out_2):
@@ -32,6 +34,7 @@ def tile_picked_trilin_none_lo_kernel(tc, xT, w1, w2, w3, w4, offs, out_0, out_1
 
     with ExitStack() as ctx:
         sb = ctx.enter_context(tc.tile_pool(name="sb", bufs=1))
+        shared = ctx.enter_context(tc.tile_pool(name="shared", bufs=1))
         ps = ctx.enter_context(tc.psum_pool(name="ps", bufs=1))
 
         x_rows = xT.rearrange("(p j) c -> p j c", j=PACK)
@@ -45,69 +48,92 @@ def tile_picked_trilin_none_lo_kernel(tc, xT, w1, w2, w3, w4, offs, out_0, out_1
                 nc.sync.dma_start(offsets[:], offs)
         w_raw = []
         for d, w in enumerate((w1, w2, w3, w4)):
-            raw = sb.tile([P, PACK, H], F32, name="w_raw%d" % d, tag="w_raw%d" % d, align_bytes=ALIGN)
-            nc.sync.dma_start(out=raw[:].rearrange("p j c -> p (j c)"), in_=w.rearrange("(p j) c -> p (j c)", j=PACK))
-            w_raw.append(raw)
+            rows = w.rearrange("(p j) c -> p j c", j=PACK)
+            parts = []
+            for m0, m1 in zip(CUTS[d][:-1], CUTS[d][1:]):
+                tag = "w_raw%d_%d" % (d, m0)
+                if d == 0:
+                    raw = shared.tile([P, PACK, H], F32, name=tag, align_bytes=ALIGN, offset=0)
+                else:
+                    raw = sb.tile([P, PACK, PACK * (m1 - m0)], F32, name=tag, tag=tag, align_bytes=ALIGN)
+                if m1 - m0 == P:
+                    nc.sync.dma_start(out=raw[:].rearrange("p j c -> p (j c)"), in_=rows.rearrange("p j c -> p (j c)"))
+                else:
+                    nc.sync.dma_start(out=raw[:], in_=rows[:, :, PACK * m0:PACK * m1])
+                parts.append((m0, m1, raw))
+            w_raw.append(parts)
 
-        picked_first = sb.tile([P, PACK, V], BF16, name="picked_first", align_bytes=ALIGN)
-        picked_rest = sb.tile([P, PACK, 2 * V], BF16, name="picked_rest", align_bytes=ALIGN)
+        picked = sb.tile([P, PACK, 2 * V], BF16, name="picked", align_bytes=ALIGN)
+        woven_first = sb.tile([P, V, PACK], BF16, name="woven_first", align_bytes=ALIGN)
+        woven_rest = {}
 
-        def gather(engine, j, d0, d1):
-            out = picked_first[:, j, :] if d0 == 0 else picked_rest[:, j, :]
-            looked_up = planes[j][:].indirect(offsets[:, 16 * d0:16 * d1])
+        def gather_first(j):
+            nc.vector.tensor_copy(out=woven_first[:, :, j], in_=planes[j][:].indirect(offsets[:, 0:V // 16]))
+
+        def gather_rest(engine, j, c0, c1):
+            looked_up = planes[j][:].indirect(offsets[:, (V + c0) // 16:(V + c1) // 16])
             if engine == "vector":
-                nc.vector.tensor_copy(out=out, in_=looked_up)
+                nc.vector.tensor_copy(out=picked[:, j, c0:c1], in_=looked_up)
             else:
-                nc.scalar.activation(out, looked_up, COPY)
+                nc.scalar.activation(picked[:, j, c0:c1], looked_up, COPY)
 
-        woven = [sb.tile([P, V, PACK], BF16, name="woven%d" % d, align_bytes=ALIGN) for d in range(3)]
+        def weave(engine, d, dst):
+            woven_rest[d] = dst
+            src = picked[:, :, (d - 1) * V:d * V]
+            copy_on(engine, woven_rest[d].rearrange("p (c i) j -> p c j i", i=4), src.rearrange("p j (c i) -> p c j i", i=4))
 
-        def weave(engine, d):
-            src = picked_first[:] if d == 0 else picked_rest[:, :, (d - 1) * V:d * V]
-            dst = woven[d][:]
-            copy_on(engine, dst.rearrange("p (c i) j -> p c j i", i=4), src.rearrange("p j (c i) -> p c j i", i=4))
+        first_words = sb.tile([P, V], U32, name="first_words", align_bytes=ALIGN)
+        first_bytes = sb.tile([P, V], U8, name="first_bytes", align_bytes=ALIGN)
+        rest_bytes = sb.tile([P, 2 * V], U8, name="rest_bytes", align_bytes=ALIGN)
+        x_codes = [first_words[:]]
+        x_scales = [first_bytes[:], rest_bytes[:, 0:V], rest_bytes[:, V:2 * V]]
 
-        x_words = sb.tile([P, S], U32, name="x_words", align_bytes=ALIGN)
-        x_bytes = sb.tile([P, S], U8, name="x_bytes", align_bytes=ALIGN)
-        x_codes = [x_words[:, d * V:(d + 1) * V] for d in range(3)]
-        x_scales = [x_bytes[:, d * V:(d + 1) * V] for d in range(3)]
+        def quantize_first():
+            nc.vector.quantize_mx(out=first_words[:].bitcast(FP8X4), scales=first_bytes[:],
+                                  in_=woven_first[:].rearrange("p c j -> p (c j)"))
 
-        def quantize_x(d):
-            nc.vector.quantize_mx(out=x_codes[d].bitcast(FP8X4), scales=x_scales[d],
-                                  in_=woven[d][:].rearrange("p c j -> p (c j)"))
+        def quantize_rest(d, words):
+            nc.vector.quantize_mx(out=words.bitcast(FP8X4), scales=x_scales[d],
+                                  in_=woven_rest[d].rearrange("p c j -> p (c j)"))
+            x_codes.append(words)
 
-        w_bf = [[None, None] for d in range(4)]
+        w_bf = [sb.tile([P, PACK, P, PACK], BF16, name="w_bf%d" % d, align_bytes=ALIGN) for d in range(4)]
         w_codes = [[sb.tile([P, 2 * P], U32, name="w_codes%d_%d" % (d, u), align_bytes=ALIGN) for u in range(2)] for d in range(4)]
         w_scales = [[sb.tile([P, 2 * P], U8, name="w_scales%d_%d" % (d, u), align_bytes=ALIGN) for u in range(2)] for d in range(4)]
 
-        def round_w(engine, d, u):
-            w_bf[d][u] = sb.tile([P, 2, P, PACK], BF16, name="w_bf%d_%d" % (d, u), tag="w_bf%d_%d" % (d, u), align_bytes=ALIGN)
-            src = w_raw[d][:].rearrange("p j (m t) -> p m j t", t=PACK)[:, :, :, 2 * u:2 * u + 2]
-            copy_on(engine, w_bf[d][u][:].rearrange("p t m j -> p m j t"), src)
+        def round_w(engine, d, m0, m1, t0=0, t1=PACK):
+            first, last, raw = [part for part in w_raw[d] if part[0] <= m0 and m1 <= part[1]][0]
+            src = raw[:].rearrange("p j (m t) -> p m j t", t=PACK)[:, m0 - first:m1 - first, :, t0:t1]
+            if engine == "gpsimd":
+                nc.gpsimd.tensor_scalar(out=w_bf[d][:, t0:t1, m0:m1, :].rearrange("p t m j -> p m t j"),
+                                        in0=src.rearrange("p m j t -> p m t j"), scalar1=1.0, scalar2=0.0, op0=MULT, op1=ADD)
+            else:
+                copy_on(engine, w_bf[d][:, t0:t1, m0:m1, :].rearrange("p t m j -> p m j t"), src)
 
-        def quantize_w(d, u):
-            nc.vector.quantize_mx(out=w_codes[d][u][:].bitcast(FP8X4), scales=w_scales[d][u][:],
-                                  in_=w_bf[d][u][:].rearrange("p t m j -> p (t m j)"))
+        def quantize_w(d, u, e0=0, e1=2):
+            cols = slice(e0 * P, e1 * P)
+            nc.vector.quantize_mx(out=w_codes[d][u][:, cols].bitcast(FP8X4), scales=w_scales[d][u][:, cols],
+                                  in_=w_bf[d][:, 2 * u + e0:2 * u + e1, :, :].rearrange("p t m j -> p (t m j)"))
 
         banks = [[ps.tile([P, PACK, HALF], F32, name="bank%d_%d" % (d, h), tag="bank%d_%d" % (d, h)) for h in range(2)] for d in range(4)]
 
-        def warm_up(tag):
-            spare = ps.tile([P, 2 * V], F32, name="spare_" + tag, tag=tag)
-            nc.tensor.matmul_mx(out=spare[:], lhsT=w_codes[2][0][:, 0:P].bitcast(FP8X4), lhsT_scale=w_scales[2][0][:, 0:P],
-                                rhs=x_words[:, 0:2 * V].bitcast(FP8X4), rhs_scale=x_bytes[:, 0:2 * V], start=True, stop=True)
+        def warm_up(c0, c1):
+            spare = banks[3][0][:].rearrange("p t v -> p (t v)")
+            nc.tensor.matmul_mx(out=spare[:, c0:c1], lhsT=w_codes[2][0][:, 0:P].bitcast(FP8X4), lhsT_scale=w_scales[2][0][:, 0:P],
+                                rhs=first_words[:, 0:c1 - c0].bitcast(FP8X4), rhs_scale=first_bytes[:, 0:c1 - c0], start=True, stop=True)
 
-        def multiply(d, u, h, codes, scales):
+        def multiply(d, u, h, codes, scales, tiles=(0, 1)):
             cols = slice(h * HALF, (h + 1) * HALF)
-            for e in range(2):
+            for e in tiles:
                 m = slice(e * P, (e + 1) * P)
                 nc.tensor.matmul_mx(out=banks[d][h][:, 2 * u + e, :],
                                     lhsT=w_codes[d][u][:, m].bitcast(FP8X4), lhsT_scale=w_scales[d][u][:, m],
                                     rhs=codes[:, cols].bitcast(FP8X4), rhs_scale=scales[:, cols],
                                     start=True, stop=True)
 
-        def first_layer(d, order):
-            for u in order:
-                for h in range(2):
+        def first_layer(d, order, halves=(0, 1)):
+            for h in halves:
+                for u in order:
                     multiply(d, u, h, x_codes[d], x_scales[d])
 
         def woven_bank(d, h):
@@ -123,8 +149,14 @@ def tile_picked_trilin_none_lo_kernel(tc, xT, w1, w2, w3, w4, offs, out_0, out_1
         r_scales = sb.tile([P, V], U8, name="r_scales", align_bytes=ALIGN)
         out_rows = out_0.rearrange("(p t) v -> p t v", t=PACK)
 
+        def first_factor(h, y1):
+            nc.scalar.copy(out=y1, in_=woven_bank(0, h))
+
+        def second_factor(h, y12, y1):
+            nc.vector.tensor_tensor(out=y12, in0=woven_bank(1, h), in1=y1, op=MULT)
+
         def last_factor(h, y12):
-            nc.vector.tensor_tensor(out=z_bf[h][:], in0=woven_bank(2, h), in1=y12[h], op=MULT)
+            nc.vector.tensor_tensor(out=z_bf[h][:], in0=woven_bank(2, h), in1=y12, op=MULT)
 
         def quantize_half(h, codes, scales, values):
             cols = slice(h * HALF, (h + 1) * HALF)
@@ -135,56 +167,65 @@ def tile_picked_trilin_none_lo_kernel(tc, xT, w1, w2, w3, w4, offs, out_0, out_1
         nc.gpsimd.memset(idle[:, 0:1], 0.0)
         nc.scalar.copy(out=idle[:, 1:2], in_=idle[:, 0:1])
 
-        gather("vector", 0, 0, 1)
-        gather("vector", 0, 1, 3)
-        gather("scalar", 1, 1, 3)
-        gather("vector", 1, 0, 1)
-        for j in (2, 3):
-            gather("scalar", j, 0, 1)
-            gather("vector", j, 1, 3)
-        weave("scalar", 0)
-        weave("vector", 1)
-        weave("vector", 2)
-        round_w("scalar", 0, 0)
-        round_w("scalar", 0, 1)
-        for d in (1, 2, 0):
-            quantize_x(d)
-        quantize_w(0, 0)
+        for j in range(PACK - 1):
+            gather_first(j)
+            gather_rest("scalar", j, 0, 2 * V)
+        gather_rest("vector", 3, V, 2 * V)
+        gather_first(3)
+        gather_rest("scalar", 3, 0, V)
+        quantize_first()
+        woven_second = sb.tile([P, V, PACK], BF16, name="woven_second", align_bytes=ALIGN)
+        weave("scalar", 1, woven_second[:])
+        round_w("scalar", 0, 0, P, 0, 2)
+        round_w("vector", 0, 0, P, 2, 4)
         quantize_w(0, 1)
-        round_w("vector", 1, 1)
-        first_layer(0, (0, 1))
-        round_w("scalar", 1, 0)
-        quantize_w(1, 0)
+        quantize_w(0, 0)
+        second_words = shared.tile([P, V], U32, name="second_words", align_bytes=ALIGN, offset=0)
+        quantize_rest(1, second_words[:])
+        first_layer(0, (1, 0))
+        woven_third = shared.tile([P, V, PACK], BF16, name="woven_third", align_bytes=ALIGN, offset=4 * V)
+        weave("scalar", 2, woven_third[:])
+        round_w("vector", 1, 0, P, 2, 4)
+        round_w("vector", 1, 0, P, 0, 2)
+        y1_tile = sb.tile([P, 2, HALF, PACK], F32, name="y1", align_bytes=ALIGN)
+        y1 = [y1_tile[:, h, :, :] for h in range(2)]
+        for h in range(2):
+            first_factor(h, y1[h])
         quantize_w(1, 1)
-        y1_first = sb.tile([P, HALF, PACK], F32, name="y1_first", tag="w_raw1", align_bytes=ALIGN)
-        nc.scalar.copy(out=y1_first[:], in_=woven_bank(0, 0))
-        round_w("vector", 2, 1)
-        first_layer(1, (0, 1))
-        round_w("scalar", 2, 0)
+        quantize_w(1, 0)
+        after_w2 = sb.tile([P, V], U32, name="after_w2", tag="w_raw1_0", align_bytes=ALIGN)
+        quantize_rest(2, after_w2[:])
+        first_layer(1, (1, 0), (1, 0))
+        round_w("vector", 2, 0, P, 2, 4)
+        round_w("vector", 2, 96, P, 0, 2)
+        round_w("scalar", 2, 0, 96, 0, 2)
         quantize_w(2, 1)
         quantize_w(2, 0)
         first_layer(2, (1, 0))
-        late = sb.tile([P, 2, HALF, PACK], F32, name="late", tag="w_raw2", align_bytes=ALIGN)
-        y12_second = sb.tile([P, HALF, PACK], F32, name="y12_second")
-        y1 = [y1_first[:], late[:, 0, :, :]]
-        y12 = [late[:, 1, :, :], y12_second[:]]
-        nc.scalar.copy(out=y1[1], in_=woven_bank(0, 1))
-        for h in range(2):
-            nc.vector.tensor_tensor(out=y12[h], in0=woven_bank(1, h), in1=y1[h], op=MULT)
-        round_w("scalar", 3, 0)
-        round_w("scalar", 3, 1)
-        last_factor(0, y12)
-        last_factor(1, y12)
-        warm_up("bank1_1")
-        warm_up("bank2_0")
+        warm_up(0, 2 * P)
+        warm_up(2 * P, 3 * P)
+        late = sb.tile([P, 3, HALF, PACK], F32, name="late", tag="w_raw2_0", align_bytes=ALIGN)
+        y12 = [late[:, h, :, :] for h in range(2)]
+        y2_part = late[:, 2, 40:HALF, :]
+        nc.scalar.copy(out=y2_part, in_=woven_bank(1, 1)[:, 40:HALF, :])
+        nc.gpsimd.tensor_tensor(out=y12[1][:, 40:HALF, :], in0=y2_part, in1=y1[1][:, 40:HALF, :], op=MULT)
+        second_factor(0, y12[0], y1[0])
+        nc.vector.tensor_tensor(out=y12[1][:, 0:40, :], in0=woven_bank(1, 1)[:, 0:40, :], in1=y1[1][:, 0:40, :], op=MULT)
+        round_w("gpsimd", 3, 80, P, 0, 2)
+        round_w("scalar", 3, 0, 80, 0, 2)
+        round_w("scalar", 3, 0, P, 2, 4)
+        last_factor(0, y12[0])
+        last_factor(1, y12[1])
         quantize_w(3, 0)
-        quantize_half(0, z_codes, z_scales, z_bf)
-        quantize_half(1, z_codes, z_scales, z_bf)
-        quantize_w(3, 1)
-        for u in range(2):
+        for h in range(2):
+            quantize_half(h, z_codes, z_scales, z_bf)
+        quantize_w(3, 1, 0, 1)
+        quantize_w(3, 1, 1, 2)
+        for h in range(2):
+            multiply(3, 0, h, z_codes, z_scales)
+        for e in range(2):
             for h in range(2):
-                multiply(3, u, h, z_codes, z_scales)
-
+                multiply(3, 1, h, z_codes, z_scales, (e,))
         nc.scalar.copy(out=result[:, :, 0:HALF], in_=banks[3][0][:])
         nc.vector.tensor_copy(out=result[:, :, HALF:V], in_=banks[3][1][:])
         nc.sync.dma_start(out=out_rows, in_=result[:])

@@ -34,7 +34,6 @@ def tile_picked_trilin_none_lo_kernel(tc, xT, w1, w2, w3, w4, offs, out_0, out_1
 
     with ExitStack() as ctx:
         sb = ctx.enter_context(tc.tile_pool(name="sb", bufs=1))
-        shared = ctx.enter_context(tc.tile_pool(name="shared", bufs=1))
         ps = ctx.enter_context(tc.psum_pool(name="ps", bufs=1))
 
         x_rows = xT.rearrange("(p j) c -> p j c", j=PACK)
@@ -52,10 +51,7 @@ def tile_picked_trilin_none_lo_kernel(tc, xT, w1, w2, w3, w4, offs, out_0, out_1
             parts = []
             for m0, m1 in zip(CUTS[d][:-1], CUTS[d][1:]):
                 tag = "w_raw%d_%d" % (d, m0)
-                if d == 0:
-                    raw = shared.tile([P, PACK, H], F32, name=tag, align_bytes=ALIGN, offset=0)
-                else:
-                    raw = sb.tile([P, PACK, PACK * (m1 - m0)], F32, name=tag, tag=tag, align_bytes=ALIGN)
+                raw = sb.tile([P, PACK, PACK * (m1 - m0)], F32, name=tag, tag=tag, align_bytes=ALIGN)
                 if m1 - m0 == P:
                     nc.sync.dma_start(out=raw[:].rearrange("p j c -> p (j c)"), in_=rows.rearrange("p j c -> p (j c)"))
                 else:
@@ -92,12 +88,7 @@ def tile_picked_trilin_none_lo_kernel(tc, xT, w1, w2, w3, w4, offs, out_0, out_1
             nc.vector.quantize_mx(out=first_words[:].bitcast(FP8X4), scales=first_bytes[:],
                                   in_=woven_first[:].rearrange("p c j -> p (c j)"))
 
-        def quantize_rest(d, words):
-            nc.vector.quantize_mx(out=words.bitcast(FP8X4), scales=x_scales[d],
-                                  in_=woven_rest[d].rearrange("p c j -> p (c j)"))
-            x_codes.append(words)
-
-        w_bf = [sb.tile([P, PACK, P, PACK], BF16, name="w_bf%d" % d, align_bytes=ALIGN) for d in range(4)]
+        w_bf = [sb.tile([P, PACK, P, PACK], BF16, name="w_bf%d" % d, tag="w_bf%d" % d, align_bytes=ALIGN) for d in range(4)]
         w_codes = [[sb.tile([P, 2 * P], U32, name="w_codes%d_%d" % (d, u), align_bytes=ALIGN) for u in range(2)] for d in range(4)]
         w_scales = [[sb.tile([P, 2 * P], U8, name="w_scales%d_%d" % (d, u), align_bytes=ALIGN) for u in range(2)] for d in range(4)]
 
@@ -143,7 +134,6 @@ def tile_picked_trilin_none_lo_kernel(tc, xT, w1, w2, w3, w4, offs, out_0, out_1
         z_codes = sb.tile([P, V], U32, name="z_codes", align_bytes=ALIGN)
         z_scales = sb.tile([P, V], U8, name="z_scales", align_bytes=ALIGN)
 
-        result = sb.tile([P, PACK, V], F32, name="result")
         r_bf = [sb.tile([P, HALF, PACK], BF16, name="r_bf%d" % h, align_bytes=ALIGN) for h in range(2)]
         r_codes = sb.tile([P, V], U32, name="r_codes", align_bytes=ALIGN)
         r_scales = sb.tile([P, V], U8, name="r_scales", align_bytes=ALIGN)
@@ -174,17 +164,18 @@ def tile_picked_trilin_none_lo_kernel(tc, xT, w1, w2, w3, w4, offs, out_0, out_1
         gather_first(3)
         gather_rest("scalar", 3, 0, V)
         quantize_first()
-        woven_second = sb.tile([P, V, PACK], BF16, name="woven_second", align_bytes=ALIGN)
-        weave("scalar", 1, woven_second[:])
+        woven_second = sb.tile([P, 2, V, PACK], BF16, name="woven_second", align_bytes=ALIGN)
+        weave("scalar", 1, woven_second[:, 0, :, :])
+        weave("vector", 2, woven_second[:, 1, :, :])
         round_w("scalar", 0, 0, P, 0, 2)
         round_w("vector", 0, 0, P, 2, 4)
         quantize_w(0, 1)
         quantize_w(0, 0)
-        second_words = shared.tile([P, V], U32, name="second_words", align_bytes=ALIGN, offset=0)
-        quantize_rest(1, second_words[:])
+        rest_words = sb.tile([P, 2 * V], U32, name="rest_words", tag="w_raw0_0", align_bytes=ALIGN)
+        nc.vector.quantize_mx(out=rest_words[:].bitcast(FP8X4), scales=rest_bytes[:],
+                              in_=woven_second[:].rearrange("p d c j -> p (d c j)"))
+        x_codes.extend([rest_words[:, 0:V], rest_words[:, V:2 * V]])
         first_layer(0, (1, 0))
-        woven_third = shared.tile([P, V, PACK], BF16, name="woven_third", align_bytes=ALIGN, offset=4 * V)
-        weave("scalar", 2, woven_third[:])
         round_w("vector", 1, 0, P, 2, 4)
         round_w("vector", 1, 0, P, 0, 2)
         y1_tile = sb.tile([P, 2, HALF, PACK], F32, name="y1", align_bytes=ALIGN)
@@ -193,8 +184,6 @@ def tile_picked_trilin_none_lo_kernel(tc, xT, w1, w2, w3, w4, offs, out_0, out_1
             first_factor(h, y1[h])
         quantize_w(1, 1)
         quantize_w(1, 0)
-        after_w2 = sb.tile([P, V], U32, name="after_w2", tag="w_raw1_0", align_bytes=ALIGN)
-        quantize_rest(2, after_w2[:])
         first_layer(1, (1, 0), (1, 0))
         round_w("vector", 2, 0, P, 2, 4)
         round_w("vector", 2, 96, P, 0, 2)
@@ -221,16 +210,30 @@ def tile_picked_trilin_none_lo_kernel(tc, xT, w1, w2, w3, w4, offs, out_0, out_1
             quantize_half(h, z_codes, z_scales, z_bf)
         quantize_w(3, 1, 0, 1)
         quantize_w(3, 1, 1, 2)
+
         for h in range(2):
             multiply(3, 0, h, z_codes, z_scales)
+        late_banks = [ps.tile([P, 2, HALF], F32, name="late_bank%d" % h, tag="bank0_%d" % h) for h in range(2)]
         for e in range(2):
+            m = slice(e * P, (e + 1) * P)
             for h in range(2):
-                multiply(3, 1, h, z_codes, z_scales, (e,))
-        nc.scalar.copy(out=result[:, :, 0:HALF], in_=banks[3][0][:])
-        nc.vector.tensor_copy(out=result[:, :, HALF:V], in_=banks[3][1][:])
-        nc.sync.dma_start(out=out_rows, in_=result[:])
-        nc.scalar.copy(out=r_bf[0][:], in_=woven_bank(3, 0))
-        nc.vector.tensor_copy(out=r_bf[1][:], in_=woven_bank(3, 1))
+                cols = slice(h * HALF, (h + 1) * HALF)
+                nc.tensor.matmul_mx(out=late_banks[h][:, e, :],
+                                    lhsT=w_codes[3][1][:, m].bitcast(FP8X4), lhsT_scale=w_scales[3][1][:, m],
+                                    rhs=z_codes[:, cols].bitcast(FP8X4), rhs_scale=z_scales[:, cols],
+                                    start=True, stop=True)
+        result = sb.tile([P, PACK, V], F32, name="result", tag="w_bf3", align_bytes=ALIGN)
+        pairs = [[banks[3][h][:, 0:2, :], late_banks[h][:]] for h in range(2)]
+        nc.scalar.copy(out=result[:, 0:2, 0:HALF], in_=pairs[0][0])
+        nc.scalar.copy(out=r_bf[0][:, :, 0:2], in_=pairs[0][0].rearrange("p t v -> p v t"))
+        nc.vector.tensor_copy(out=result[:, 0:2, HALF:V], in_=pairs[1][0])
+        nc.sync.dma_start(out=out_rows[:, 0:2, :], in_=result[:, 0:2, :])
+        nc.scalar.copy(out=result[:, 2:4, 0:HALF], in_=pairs[0][1])
+        nc.vector.tensor_copy(out=result[:, 2:4, HALF:V], in_=pairs[1][1])
+        nc.sync.dma_start(out=out_rows[:, 2:4, :], in_=result[:, 2:4, :])
+        nc.scalar.copy(out=r_bf[0][:, :, 2:4], in_=pairs[0][1].rearrange("p t v -> p v t"))
+        nc.vector.tensor_copy(out=r_bf[1][:].rearrange("p (c i) t -> p c t i", i=4),
+                              in_=result[:, :, HALF:V].rearrange("p t (c i) -> p c t i", i=4))
         for h in range(2):
             quantize_half(h, r_codes, r_scales, r_bf)
         words = out_1.rearrange("z p c r -> (z p) (c r)").bitcast(I32)

@@ -109,7 +109,6 @@ def tile_picked_trilin_none_lo_kernel(tc, xT, w1, w2, w3, w4, offs, out_0, out_1
         banks = [[ps.tile([P, PACK, HALF], F32, name="bank%d_%d" % (d, h), tag="bank%d_%d" % (d, h)) for h in range(2)] for d in range(4)]
 
         def warm_up(c0, c1):
-            spare = banks[3][0][:].rearrange("p t v -> p (t v)")
             nc.tensor.matmul_mx(out=spare[:, c0:c1], lhsT=w_codes[2][0][:, 0:P].bitcast(FP8X4), lhsT_scale=w_scales[2][0][:, 0:P],
                                 rhs=first_words[:, 0:c1 - c0].bitcast(FP8X4), rhs_scale=first_bytes[:, 0:c1 - c0], start=True, stop=True)
 
@@ -191,8 +190,6 @@ def tile_picked_trilin_none_lo_kernel(tc, xT, w1, w2, w3, w4, offs, out_0, out_1
         quantize_w(2, 1)
         quantize_w(2, 0)
         first_layer(2, (1, 0))
-        warm_up(0, 2 * P)
-        warm_up(2 * P, 3 * P)
         late = sb.tile([P, 3, HALF, PACK], F32, name="late", tag="w_raw2_0", align_bytes=ALIGN)
         y12 = [late[:, h, :, :] for h in range(2)]
         y2_part = late[:, 2, 40:HALF, :]
@@ -204,6 +201,9 @@ def tile_picked_trilin_none_lo_kernel(tc, xT, w1, w2, w3, w4, offs, out_0, out_1
         round_w("scalar", 3, 0, 80, 0, 2)
         round_w("scalar", 3, 0, P, 2, 4)
         last_factor(0, y12[0])
+        spare = ps.tile([P, 3 * P], F32, name="spare", tag="bank2_0")
+        warm_up(0, 2 * P)
+        warm_up(2 * P, 3 * P)
         last_factor(1, y12[1])
         quantize_w(3, 0)
         for h in range(2):

@@ -197,8 +197,8 @@ def tile_picked_trilin_none_lo_kernel(tc, xT, w1, w2, w3, w4, offs, out_0, out_1
         nc.gpsimd.tensor_tensor(out=y12[1][:, 40:HALF, :], in0=y2_part, in1=y1[1][:, 40:HALF, :], op=MULT)
         second_factor(0, y12[0], y1[0])
         nc.vector.tensor_tensor(out=y12[1][:, 0:40, :], in0=woven_bank(1, 1)[:, 0:40, :], in1=y1[1][:, 0:40, :], op=MULT)
-        round_w("gpsimd", 3, 80, P, 0, 2)
-        round_w("scalar", 3, 0, 80, 0, 2)
+        round_w("gpsimd", 3, 70, P, 0, 2)
+        round_w("scalar", 3, 0, 70, 0, 2)
         round_w("scalar", 3, 0, P, 2, 4)
         last_factor(0, y12[0])
         spare = ps.tile([P, 3 * P], F32, name="spare", tag="bank2_0")
@@ -216,7 +216,7 @@ def tile_picked_trilin_none_lo_kernel(tc, xT, w1, w2, w3, w4, offs, out_0, out_1
         late_banks = [ps.tile([P, 2, HALF], F32, name="late_bank%d" % h, tag="bank0_%d" % h) for h in range(2)]
         for e in range(2):
             m = slice(e * P, (e + 1) * P)
-            for h in range(2):
+            for h in (1, 0):
                 cols = slice(h * HALF, (h + 1) * HALF)
                 nc.tensor.matmul_mx(out=late_banks[h][:, e, :],
                                     lhsT=w_codes[3][1][:, m].bitcast(FP8X4), lhsT_scale=w_scales[3][1][:, m],

@@ -14,13 +14,15 @@ U8 = mybir.dt.uint8
 FP8X4 = mybir.dt.float8_e4m3fn_x4
 MULT = mybir.AluOpType.mult
 ADD = mybir.AluOpType.add
+COPY = mybir.ActivationFunctionType.Copy
 
 P = 128
 PACK = 4
 HALF = V // 2
 ALIGN = 64
-COPY = mybir.ActivationFunctionType.Copy
-CUTS = ((0, 128), (0, 128), (0, 128), (0, 128))
+SCALAR_SHARE = 96
+VECTOR_TRIPLES = 64
+GPSIMD_FROM = 88
 
 
 def tile_picked_trilin_none_lo_kernel(tc, xT, w1, w2, w3, w4, offs, out_0, out_1, out_2):
@@ -47,24 +49,15 @@ def tile_picked_trilin_none_lo_kernel(tc, xT, w1, w2, w3, w4, offs, out_0, out_1
                 nc.sync.dma_start(offsets[:], offs)
         w_raw = []
         for d, w in enumerate((w1, w2, w3, w4)):
-            rows = w.rearrange("(p j) c -> p j c", j=PACK)
-            parts = []
-            for m0, m1 in zip(CUTS[d][:-1], CUTS[d][1:]):
-                tag = "w_raw%d_%d" % (d, m0)
-                raw = sb.tile([P, PACK, PACK * (m1 - m0)], F32, name=tag, tag=tag, align_bytes=ALIGN)
-                if m1 - m0 == P:
-                    nc.sync.dma_start(out=raw[:].rearrange("p j c -> p (j c)"), in_=rows.rearrange("p j c -> p (j c)"))
-                else:
-                    nc.sync.dma_start(out=raw[:], in_=rows[:, :, PACK * m0:PACK * m1])
-                parts.append((m0, m1, raw))
-            w_raw.append(parts)
+            raw = sb.tile([P, PACK, H], F32, name="w_raw%d" % d, tag="w_raw%d" % d, align_bytes=ALIGN)
+            nc.sync.dma_start(out=raw[:].rearrange("p j c -> p (j c)"), in_=w.rearrange("(p j) c -> p (j c)", j=PACK))
+            w_raw.append(raw)
 
         picked = sb.tile([P, PACK, 2 * V], BF16, name="picked", align_bytes=ALIGN)
-        woven_first = sb.tile([P, V, PACK], BF16, name="woven_first", align_bytes=ALIGN)
-        woven_rest = {}
+        woven = [sb.tile([P, V, PACK], BF16, name="woven%d" % d, align_bytes=ALIGN) for d in range(3)]
 
         def gather_first(j):
-            nc.vector.tensor_copy(out=woven_first[:, :, j], in_=planes[j][:].indirect(offsets[:, 0:V // 16]))
+            nc.vector.tensor_copy(out=woven[0][:, :, j], in_=planes[j][:].indirect(offsets[:, 0:V // 16]))
 
         def gather_rest(engine, j, c0, c1):
             looked_up = planes[j][:].indirect(offsets[:, (V + c0) // 16:(V + c1) // 16])
@@ -73,79 +66,61 @@ def tile_picked_trilin_none_lo_kernel(tc, xT, w1, w2, w3, w4, offs, out_0, out_1
             else:
                 nc.scalar.activation(picked[:, j, c0:c1], looked_up, COPY)
 
-        def weave(engine, d, dst):
-            woven_rest[d] = dst
+        def weave(engine, d):
             src = picked[:, :, (d - 1) * V:d * V]
-            copy_on(engine, woven_rest[d].rearrange("p (c i) j -> p c j i", i=4), src.rearrange("p j (c i) -> p c j i", i=4))
+            copy_on(engine, woven[d][:].rearrange("p (c i) j -> p c j i", i=4), src.rearrange("p j (c i) -> p c j i", i=4))
 
-        first_words = sb.tile([P, V], U32, name="first_words", align_bytes=ALIGN)
-        first_bytes = sb.tile([P, V], U8, name="first_bytes", align_bytes=ALIGN)
-        rest_bytes = sb.tile([P, 2 * V], U8, name="rest_bytes", align_bytes=ALIGN)
-        x_codes = [first_words[:]]
-        x_scales = [first_bytes[:], rest_bytes[:, 0:V], rest_bytes[:, V:2 * V]]
+        x_codes = {}
+        x_scales = [sb.tile([P, V], U8, name="x_scales%d" % d, align_bytes=ALIGN) for d in range(3)]
 
-        def quantize_first():
-            nc.vector.quantize_mx(out=first_words[:].bitcast(FP8X4), scales=first_bytes[:],
-                                  in_=woven_first[:].rearrange("p c j -> p (c j)"))
+        def quantize_x(d, tag):
+            x_codes[d] = sb.tile([P, V], U32, name="x_codes%d" % d, tag=tag, align_bytes=ALIGN)
+            nc.vector.quantize_mx(out=x_codes[d][:].bitcast(FP8X4), scales=x_scales[d][:],
+                                  in_=woven[d][:].rearrange("p c j -> p (c j)"))
 
-        w_bf = [sb.tile([P, PACK, P, PACK], BF16, name="w_bf%d" % d, tag="w_bf%d" % d, align_bytes=ALIGN) for d in range(4)]
+        w_bf = {d: sb.tile([P, PACK, P, PACK], BF16, name="w_bf%d" % d, tag="w_bf%d" % d, align_bytes=ALIGN) for d in (0, 1, 3)}
+        third_bf = [sb.tile([P, 2, P, PACK], BF16, name="third_bf%d" % u, tag="third_bf%d" % u, align_bytes=ALIGN) for u in range(2)]
+
+        def rounded(d, u):
+            if d == 2:
+                return third_bf[u][:]
+            return w_bf[d][:] if u is None else w_bf[d][:, 2 * u:2 * u + 2, :, :]
+
         w_codes = [[sb.tile([P, 2 * P], U32, name="w_codes%d_%d" % (d, u), align_bytes=ALIGN) for u in range(2)] for d in range(4)]
         w_scales = [[sb.tile([P, 2 * P], U8, name="w_scales%d_%d" % (d, u), align_bytes=ALIGN) for u in range(2)] for d in range(4)]
 
-        def round_w(engine, d, m0, m1, t0=0, t1=PACK):
-            first, last, raw = [part for part in w_raw[d] if part[0] <= m0 and m1 <= part[1]][0]
-            src = raw[:].rearrange("p j (m t) -> p m j t", t=PACK)[:, m0 - first:m1 - first, :, t0:t1]
+        def round_w(engine, d, u, m0, m1):
+            tiles = slice(0, PACK) if u is None else slice(2 * u, 2 * u + 2)
+            src = w_raw[d][:].rearrange("p j (m t) -> p m j t", t=PACK)[:, m0:m1, :, tiles]
+            dst = rounded(d, u)[:, :, m0:m1, :]
             if engine == "gpsimd":
-                nc.gpsimd.tensor_scalar(out=w_bf[d][:, t0:t1, m0:m1, :].rearrange("p t m j -> p m t j"),
-                                        in0=src.rearrange("p m j t -> p m t j"), scalar1=1.0, scalar2=0.0, op0=MULT, op1=ADD)
+                nc.gpsimd.tensor_scalar(out=dst.rearrange("p t m j -> p m t j"), in0=src.rearrange("p m j t -> p m t j"),
+                                        scalar1=1.0, scalar2=0.0, op0=MULT, op1=ADD)
             else:
-                copy_on(engine, w_bf[d][:, t0:t1, m0:m1, :].rearrange("p t m j -> p m j t"), src)
+                copy_on(engine, dst.rearrange("p t m j -> p m j t"), src)
 
         def quantize_w(d, u, e0=0, e1=2):
             cols = slice(e0 * P, e1 * P)
             nc.vector.quantize_mx(out=w_codes[d][u][:, cols].bitcast(FP8X4), scales=w_scales[d][u][:, cols],
-                                  in_=w_bf[d][:, 2 * u + e0:2 * u + e1, :, :].rearrange("p t m j -> p (t m j)"))
+                                  in_=rounded(d, u)[:, e0:e1, :, :].rearrange("p t m j -> p (t m j)"))
 
-        banks = [[ps.tile([P, PACK, HALF], F32, name="bank%d_%d" % (d, h), tag="bank%d_%d" % (d, h)) for h in range(2)] for d in range(4)]
+        def bank(name, tag, tiles):
+            return ps.tile([P, tiles, HALF], F32, name=name, tag="bank%d" % tag)
 
-        def warm_up(c0, c1):
-            nc.tensor.matmul_mx(out=spare[:, c0:c1], lhsT=w_codes[2][0][:, 0:P].bitcast(FP8X4), lhsT_scale=w_scales[2][0][:, 0:P],
-                                rhs=first_words[:, 0:c1 - c0].bitcast(FP8X4), rhs_scale=first_bytes[:, 0:c1 - c0], start=True, stop=True)
-
-        def multiply(d, u, h, codes, scales, tiles=(0, 1)):
+        def one_pass(out, d, u, e, codes, scales, h):
             cols = slice(h * HALF, (h + 1) * HALF)
-            for e in tiles:
-                m = slice(e * P, (e + 1) * P)
-                nc.tensor.matmul_mx(out=banks[d][h][:, 2 * u + e, :],
-                                    lhsT=w_codes[d][u][:, m].bitcast(FP8X4), lhsT_scale=w_scales[d][u][:, m],
-                                    rhs=codes[:, cols].bitcast(FP8X4), rhs_scale=scales[:, cols],
-                                    start=True, stop=True)
+            m = slice(e * P, (e + 1) * P)
+            nc.tensor.matmul_mx(out=out, lhsT=w_codes[d][u][:, m].bitcast(FP8X4), lhsT_scale=w_scales[d][u][:, m],
+                                rhs=codes[:, cols].bitcast(FP8X4), rhs_scale=scales[:, cols], start=True, stop=True)
 
-        def first_layer(d, order, halves=(0, 1)):
-            for h in halves:
-                for u in order:
-                    multiply(d, u, h, x_codes[d], x_scales[d])
+        y = {}
 
-        def woven_bank(d, h):
-            return banks[d][h][:].rearrange("p t v -> p v t")
-
-        z_bf = [sb.tile([P, HALF, PACK], BF16, name="z_bf%d" % h, align_bytes=ALIGN) for h in range(2)]
-        z_codes = sb.tile([P, V], U32, name="z_codes", align_bytes=ALIGN)
-        z_scales = sb.tile([P, V], U8, name="z_scales", align_bytes=ALIGN)
-
-        r_bf = [sb.tile([P, HALF, PACK], BF16, name="r_bf%d" % h, align_bytes=ALIGN) for h in range(2)]
-        r_codes = sb.tile([P, V], U32, name="r_codes", align_bytes=ALIGN)
-        r_scales = sb.tile([P, V], U8, name="r_scales", align_bytes=ALIGN)
-        out_rows = out_0.rearrange("(p t) v -> p t v", t=PACK)
-
-        def first_factor(h, y1):
-            nc.scalar.copy(out=y1, in_=woven_bank(0, h))
-
-        def second_factor(h, y12, y1):
-            nc.vector.tensor_tensor(out=y12, in0=woven_bank(1, h), in1=y1, op=MULT)
-
-        def last_factor(h, y12):
-            nc.vector.tensor_tensor(out=z_bf[h][:], in0=woven_bank(2, h), in1=y12, op=MULT)
+        def first_layer(d, h, tag):
+            target = bank("y%d_%d" % (d, h), tag, PACK)
+            for u in (1, 0):
+                for e in range(2):
+                    one_pass(target[:, 2 * u + e, :], d, u, e, x_codes[d], x_scales[d], h)
+            y[d, h] = target[:].rearrange("p t v -> p v t")
 
         def quantize_half(h, codes, scales, values):
             cols = slice(h * HALF, (h + 1) * HALF)
@@ -162,76 +137,95 @@ def tile_picked_trilin_none_lo_kernel(tc, xT, w1, w2, w3, w4, offs, out_0, out_1
         gather_rest("vector", 3, V, 2 * V)
         gather_first(3)
         gather_rest("scalar", 3, 0, V)
-        quantize_first()
-        woven_second = sb.tile([P, 2, V, PACK], BF16, name="woven_second", align_bytes=ALIGN)
-        weave("scalar", 1, woven_second[:, 0, :, :])
-        weave("vector", 2, woven_second[:, 1, :, :])
-        round_w("scalar", 0, 0, P, 0, 2)
-        round_w("vector", 0, 0, P, 2, 4)
+        quantize_x(0, "x_codes0")
+        weave("scalar", 1)
+        weave("vector", 2)
+
+        round_w("scalar", 0, 0, 0, P)
+        round_w("vector", 0, 1, 0, P)
         quantize_w(0, 1)
+        quantize_x(1, "w_raw0")
         quantize_w(0, 0)
-        rest_words = sb.tile([P, 2 * V], U32, name="rest_words", tag="w_raw0_0", align_bytes=ALIGN)
-        nc.vector.quantize_mx(out=rest_words[:].bitcast(FP8X4), scales=rest_bytes[:],
-                              in_=woven_second[:].rearrange("p d c j -> p (d c j)"))
-        x_codes.extend([rest_words[:, 0:V], rest_words[:, V:2 * V]])
-        first_layer(0, (1, 0))
-        round_w("vector", 1, 0, P, 2, 4)
-        round_w("vector", 1, 0, P, 0, 2)
-        y1_tile = sb.tile([P, 2, HALF, PACK], F32, name="y1", align_bytes=ALIGN)
-        y1 = [y1_tile[:, h, :, :] for h in range(2)]
         for h in range(2):
-            first_factor(h, y1[h])
+            first_layer(0, h, h)
+
+        round_w("vector", 1, 1, 40, P)
+        round_w("vector", 1, 0, 40, P)
+        round_w("scalar", 1, None, 0, 40)
+        y1 = [w_raw[1][:, :, h * HALF:(h + 1) * HALF].rearrange("p j (v t) -> p j v t", t=PACK) for h in range(2)]
+        for h in range(2):
+            nc.scalar.copy(out=y1[h], in_=y[0, h].rearrange("p (j v) t -> p j v t", j=PACK))
         quantize_w(1, 1)
         quantize_w(1, 0)
-        first_layer(1, (1, 0), (1, 0))
-        round_w("vector", 2, 0, P, 2, 4)
-        round_w("vector", 2, 96, P, 0, 2)
-        round_w("scalar", 2, 0, 96, 0, 2)
+        quantize_x(2, "w_bf0")
+        first_layer(1, 1, 0)
+        first_layer(1, 0, 1)
+
+        round_w("vector", 2, 1, 0, P)
+        round_w("vector", 2, 0, SCALAR_SHARE, P)
+        round_w("scalar", 2, 0, 0, 32)
+        round_w("scalar", 2, 0, 32, SCALAR_SHARE)
         quantize_w(2, 1)
         quantize_w(2, 0)
-        first_layer(2, (1, 0))
-        late = sb.tile([P, 3, HALF, PACK], F32, name="late", tag="w_raw2_0", align_bytes=ALIGN)
-        y12 = [late[:, h, :, :] for h in range(2)]
-        y2_part = late[:, 2, 40:HALF, :]
-        nc.scalar.copy(out=y2_part, in_=woven_bank(1, 1)[:, 40:HALF, :])
-        nc.gpsimd.tensor_tensor(out=y12[1][:, 40:HALF, :], in0=y2_part, in1=y1[1][:, 40:HALF, :], op=MULT)
-        second_factor(0, y12[0], y1[0])
-        nc.vector.tensor_tensor(out=y12[1][:, 0:40, :], in0=woven_bank(1, 1)[:, 0:40, :], in1=y1[1][:, 0:40, :], op=MULT)
-        round_w("gpsimd", 3, 70, P, 0, 2)
-        round_w("scalar", 3, 0, 70, 0, 2)
-        round_w("scalar", 3, 0, P, 2, 4)
-        last_factor(0, y12[0])
-        spare = ps.tile([P, 3 * P], F32, name="spare", tag="bank2_0")
-        warm_up(0, 2 * P)
-        warm_up(2 * P, 3 * P)
-        last_factor(1, y12[1])
-        quantize_w(3, 0)
+        for h in range(2):
+            first_layer(2, h, 2 + h)
+
+        def by_rows(values):
+            return values.rearrange("p (j v) t -> p j v t", v=32)
+
+        y12_first = w_raw[2][:, :, P:2 * P].rearrange("p j (v t) -> p j v t", t=PACK)
+        y12_second = sb.tile([P, HALF, PACK], F32, name="y12_second", tag="third_bf1", align_bytes=ALIGN)
+        rows_from = VECTOR_TRIPLES // 32
+        y2_part = w_raw[2][:, rows_from:PACK, 0:P].rearrange("p j (v t) -> p j v t", t=PACK)
+        nc.scalar.copy(out=y2_part, in_=by_rows(y[1, 1][:, VECTOR_TRIPLES:HALF, :]))
+        nc.gpsimd.tensor_tensor(out=by_rows(y12_second[:, VECTOR_TRIPLES:HALF, :]), in0=y2_part, in1=y1[1][:, rows_from:PACK, :, :], op=MULT)
+        nc.vector.tensor_tensor(out=y12_first, in0=by_rows(y[1, 0]), in1=y1[0], op=MULT)
+        nc.vector.tensor_tensor(out=by_rows(y12_second[:, 0:VECTOR_TRIPLES, :]), in0=by_rows(y[1, 1][:, 0:VECTOR_TRIPLES, :]),
+                                in1=y1[1][:, 0:rows_from, :, :], op=MULT)
+        round_w("gpsimd", 3, None, GPSIMD_FROM, P)
+        round_w("scalar", 3, 0, 0, GPSIMD_FROM)
+        round_w("scalar", 3, 1, 0, GPSIMD_FROM)
+
+        z_bf = [sb.tile([P, HALF, PACK], BF16, name="z_bf%d" % h, align_bytes=ALIGN) for h in range(2)]
+        z_codes = sb.tile([P, V], U32, name="z_codes", align_bytes=ALIGN)
+        z_scales = sb.tile([P, V], U8, name="z_scales", align_bytes=ALIGN)
+        nc.vector.tensor_tensor(out=by_rows(z_bf[0][:]), in0=by_rows(y[2, 0]), in1=y12_first, op=MULT)
+        spare = ps.tile([P, 3 * P], F32, name="spare", tag="bank2")
+        for c0, c1 in ((0, 2 * P), (2 * P, 3 * P)):
+            nc.tensor.matmul_mx(out=spare[:, c0:c1], lhsT=w_codes[2][0][:, 0:P].bitcast(FP8X4), lhsT_scale=w_scales[2][0][:, 0:P],
+                                rhs=x_codes[0][:, 0:c1 - c0].bitcast(FP8X4), rhs_scale=x_scales[0][:, 0:c1 - c0], start=True, stop=True)
+        nc.vector.tensor_tensor(out=z_bf[1][:], in0=y[2, 1], in1=y12_second[:], op=MULT)
         for h in range(2):
             quantize_half(h, z_codes, z_scales, z_bf)
-        quantize_w(3, 1, 0, 1)
-        quantize_w(3, 1, 1, 2)
+        for u in range(2):
+            for e in range(2):
+                quantize_w(3, u, e, e + 1)
 
-        for h in range(2):
-            multiply(3, 0, h, z_codes, z_scales)
-        late_banks = [ps.tile([P, 2, HALF], F32, name="late_bank%d" % h, tag="bank0_%d" % h) for h in range(2)]
+        early = [bank("early%d" % h, 4 + h, 2) for h in range(2)]
         for e in range(2):
-            m = slice(e * P, (e + 1) * P)
+            for h in range(2):
+                one_pass(early[h][:, e, :], 3, 0, e, z_codes, z_scales, h)
+        last = [bank("last%d" % h, 6 + h, 2) for h in range(2)]
+        for e in range(2):
             for h in (1, 0):
-                cols = slice(h * HALF, (h + 1) * HALF)
-                nc.tensor.matmul_mx(out=late_banks[h][:, e, :],
-                                    lhsT=w_codes[3][1][:, m].bitcast(FP8X4), lhsT_scale=w_scales[3][1][:, m],
-                                    rhs=z_codes[:, cols].bitcast(FP8X4), rhs_scale=z_scales[:, cols],
-                                    start=True, stop=True)
+                one_pass(last[h][:, e, :], 3, 1, e, z_codes, z_scales, h)
+        twin = bank("twin", 1, 2)
+        for e in range(2):
+            one_pass(twin[:, e, :], 3, 1, e, z_codes, z_scales, 0)
+
+        r_bf = [sb.tile([P, HALF, PACK], BF16, name="r_bf%d" % h, align_bytes=ALIGN) for h in range(2)]
+        r_codes = sb.tile([P, V], U32, name="r_codes", align_bytes=ALIGN)
+        r_scales = sb.tile([P, V], U8, name="r_scales", align_bytes=ALIGN)
+        out_rows = out_0.rearrange("(p t) v -> p t v", t=PACK)
         result = sb.tile([P, PACK, V], F32, name="result", tag="w_bf3", align_bytes=ALIGN)
-        pairs = [[banks[3][h][:, 0:2, :], late_banks[h][:]] for h in range(2)]
-        nc.scalar.copy(out=result[:, 0:2, 0:HALF], in_=pairs[0][0])
-        nc.scalar.copy(out=r_bf[0][:, :, 0:2], in_=pairs[0][0].rearrange("p t v -> p v t"))
-        nc.vector.tensor_copy(out=result[:, 0:2, HALF:V], in_=pairs[1][0])
+        nc.scalar.copy(out=result[:, 0:2, 0:HALF], in_=early[0][:])
+        nc.scalar.copy(out=r_bf[0][:, :, 0:2], in_=early[0][:].rearrange("p t v -> p v t"))
+        nc.vector.tensor_copy(out=result[:, 0:2, HALF:V], in_=early[1][:])
         nc.sync.dma_start(out=out_rows[:, 0:2, :], in_=result[:, 0:2, :])
-        nc.scalar.copy(out=result[:, 2:4, 0:HALF], in_=pairs[0][1])
-        nc.vector.tensor_copy(out=result[:, 2:4, HALF:V], in_=pairs[1][1])
+        nc.scalar.copy(out=r_bf[0][:, :, 2:4], in_=last[0][:].rearrange("p t v -> p v t"))
+        nc.vector.tensor_copy(out=result[:, 2:4, HALF:V], in_=last[1][:])
+        nc.vector.tensor_copy(out=result[:, 2:4, 0:HALF], in_=twin[:])
         nc.sync.dma_start(out=out_rows[:, 2:4, :], in_=result[:, 2:4, :])
-        nc.scalar.copy(out=r_bf[0][:, :, 2:4], in_=pairs[0][1].rearrange("p t v -> p v t"))
         nc.vector.tensor_copy(out=r_bf[1][:].rearrange("p (c i) t -> p c t i", i=4),
                               in_=result[:, :, HALF:V].rearrange("p t (c i) -> p c t i", i=4))
         for h in range(2):

@@ -22,7 +22,7 @@ HALF = V // 2
 ALIGN = 64
 SCALAR_SHARE = 96
 VECTOR_TRIPLES = 64
-GPSIMD_FROM = 88
+GPSIMD_FROM = 96
 
 
 def tile_picked_trilin_none_lo_kernel(tc, xT, w1, w2, w3, w4, offs, out_0, out_1, out_2):
@@ -195,15 +195,14 @@ def tile_picked_trilin_none_lo_kernel(tc, xT, w1, w2, w3, w4, offs, out_0, out_1
             nc.tensor.matmul_mx(out=spare[:, c0:c1], lhsT=w_codes[2][0][:, 0:P].bitcast(FP8X4), lhsT_scale=w_scales[2][0][:, 0:P],
                                 rhs=x_codes[0][:, 0:c1 - c0].bitcast(FP8X4), rhs_scale=x_scales[0][:, 0:c1 - c0], start=True, stop=True)
         nc.vector.tensor_tensor(out=z_bf[1][:], in0=y[2, 1], in1=y12_second[:], op=MULT)
-        for h in range(2):
-            quantize_half(h, z_codes, z_scales, z_bf)
         for u in range(2):
+            quantize_half(u, z_codes, z_scales, z_bf)
             for e in range(2):
                 quantize_w(3, u, e, e + 1)
 
         early = [bank("early%d" % h, 4 + h, 2) for h in range(2)]
-        for e in range(2):
-            for h in range(2):
+        for h in range(2):
+            for e in range(2):
                 one_pass(early[h][:, e, :], 3, 0, e, z_codes, z_scales, h)
         last = [bank("last%d" % h, 6 + h, 2) for h in range(2)]
         for e in range(2):

@@ -23,6 +23,8 @@ ALIGN = 64
 SCALAR_SHARE = 96
 VECTOR_TRIPLES = 64
 GPSIMD_FROM = 96
+EDGE = 20
+MARGIN = H - 64
 
 
 def tile_picked_trilin_none_lo_kernel(tc, xT, w1, w2, w3, w4, offs, out_0, out_1, out_2):
@@ -48,10 +50,13 @@ def tile_picked_trilin_none_lo_kernel(tc, xT, w1, w2, w3, w4, offs, out_0, out_1
             if j == 0:
                 nc.sync.dma_start(offsets[:], offs)
         w_raw = []
+        rooms = []
         for d, w in enumerate((w1, w2, w3, w4)):
-            raw = sb.tile([P, PACK, H], F32, name="w_raw%d" % d, tag="w_raw%d" % d, align_bytes=ALIGN)
-            nc.sync.dma_start(out=raw[:].rearrange("p j c -> p (j c)"), in_=w.rearrange("(p j) c -> p (j c)", j=PACK))
-            w_raw.append(raw)
+            pad = MARGIN if d == 1 else 0
+            room = sb.tile([P, PACK * H + 2 * pad], F32, name="w_raw%d" % d, tag="w_raw%d" % d, align_bytes=ALIGN)
+            nc.sync.dma_start(out=room[:, pad:pad + PACK * H], in_=w.rearrange("(p j) c -> p (j c)", j=PACK))
+            w_raw.append(room[:, pad:pad + PACK * H].rearrange("p (j c) -> p j c", j=PACK))
+            rooms.append(room)
 
         picked = sb.tile([P, PACK, 2 * V], BF16, name="picked", align_bytes=ALIGN)
         woven = [sb.tile([P, V, PACK], BF16, name="woven%d" % d, align_bytes=ALIGN) for d in range(3)]
@@ -91,7 +96,7 @@ def tile_picked_trilin_none_lo_kernel(tc, xT, w1, w2, w3, w4, offs, out_0, out_1
 
         def round_w(engine, d, u, m0, m1):
             tiles = slice(0, PACK) if u is None else slice(2 * u, 2 * u + 2)
-            src = w_raw[d][:].rearrange("p j (m t) -> p m j t", t=PACK)[:, m0:m1, :, tiles]
+            src = w_raw[d].rearrange("p j (m t) -> p m j t", t=PACK)[:, m0:m1, :, tiles]
             dst = rounded(d, u)[:, :, m0:m1, :]
             if engine == "gpsimd":
                 nc.gpsimd.tensor_scalar(out=dst.rearrange("p t m j -> p m t j"), in0=src.rearrange("p m j t -> p m t j"),
@@ -144,17 +149,19 @@ def tile_picked_trilin_none_lo_kernel(tc, xT, w1, w2, w3, w4, offs, out_0, out_1
         round_w("scalar", 0, 0, 0, P)
         round_w("vector", 0, 1, 0, P)
         quantize_w(0, 1)
-        quantize_x(1, "w_raw0")
         quantize_w(0, 0)
+        quantize_x(1, "w_raw0")
         for h in range(2):
             first_layer(0, h, h)
 
-        round_w("vector", 1, 1, 40, P)
-        round_w("vector", 1, 0, 40, P)
-        round_w("scalar", 1, None, 0, 40)
-        y1 = [w_raw[1][:, :, h * HALF:(h + 1) * HALF].rearrange("p j (v t) -> p j v t", t=PACK) for h in range(2)]
+        round_w("vector", 1, 1, EDGE, P - EDGE)
+        round_w("vector", 1, 0, EDGE, P - EDGE)
+        round_w("scalar", 1, None, 0, EDGE)
+        round_w("scalar", 1, None, P - EDGE, P)
+        ends = (rooms[1][:, 0:H], rooms[1][:, PACK * H + 2 * MARGIN - H:PACK * H + 2 * MARGIN])
+        y1 = [end.rearrange("p (v t) -> p v t", t=PACK) for end in ends]
         for h in range(2):
-            nc.scalar.copy(out=y1[h], in_=y[0, h].rearrange("p (j v) t -> p j v t", j=PACK))
+            nc.scalar.copy(out=y1[h], in_=y[0, h])
         quantize_w(1, 1)
         quantize_w(1, 0)
         quantize_x(2, "w_bf0")
@@ -163,25 +170,21 @@ def tile_picked_trilin_none_lo_kernel(tc, xT, w1, w2, w3, w4, offs, out_0, out_1
 
         round_w("vector", 2, 1, 0, P)
         round_w("vector", 2, 0, SCALAR_SHARE, P)
-        round_w("scalar", 2, 0, 0, 32)
-        round_w("scalar", 2, 0, 32, SCALAR_SHARE)
+        round_w("scalar", 2, 0, 0, 64)
+        round_w("scalar", 2, 0, 64, SCALAR_SHARE)
         quantize_w(2, 1)
         quantize_w(2, 0)
         for h in range(2):
             first_layer(2, h, 2 + h)
 
-        def by_rows(values):
-            return values.rearrange("p (j v) t -> p j v t", v=32)
-
-        y12_first = w_raw[2][:, :, P:2 * P].rearrange("p j (v t) -> p j v t", t=PACK)
-        y12_second = sb.tile([P, HALF, PACK], F32, name="y12_second", tag="third_bf1", align_bytes=ALIGN)
-        rows_from = VECTOR_TRIPLES // 32
-        y2_part = w_raw[2][:, rows_from:PACK, 0:P].rearrange("p j (v t) -> p j v t", t=PACK)
-        nc.scalar.copy(out=y2_part, in_=by_rows(y[1, 1][:, VECTOR_TRIPLES:HALF, :]))
-        nc.gpsimd.tensor_tensor(out=by_rows(y12_second[:, VECTOR_TRIPLES:HALF, :]), in0=y2_part, in1=y1[1][:, rows_from:PACK, :, :], op=MULT)
-        nc.vector.tensor_tensor(out=y12_first, in0=by_rows(y[1, 0]), in1=y1[0], op=MULT)
-        nc.vector.tensor_tensor(out=by_rows(y12_second[:, 0:VECTOR_TRIPLES, :]), in0=by_rows(y[1, 1][:, 0:VECTOR_TRIPLES, :]),
-                                in1=y1[1][:, 0:rows_from, :, :], op=MULT)
+        second = sb.tile([P, HALF, PACK], F32, name="second", tag="third_bf1", align_bytes=ALIGN)
+        y12 = [w_raw[2][:, PACK - 1, :].rearrange("p (v t) -> p v t", t=PACK), second[:]]
+        y2_part = w_raw[2][:, 0, 0:PACK * (HALF - VECTOR_TRIPLES)].rearrange("p (v t) -> p v t", t=PACK)
+        nc.scalar.copy(out=y2_part, in_=y[1, 1][:, VECTOR_TRIPLES:HALF, :])
+        nc.gpsimd.tensor_tensor(out=y12[1][:, VECTOR_TRIPLES:HALF, :], in0=y2_part, in1=y1[1][:, VECTOR_TRIPLES:HALF, :], op=MULT)
+        nc.vector.tensor_tensor(out=y12[0], in0=y[1, 0], in1=y1[0], op=MULT)
+        nc.vector.tensor_tensor(out=y12[1][:, 0:VECTOR_TRIPLES, :], in0=y[1, 1][:, 0:VECTOR_TRIPLES, :],
+                                in1=y1[1][:, 0:VECTOR_TRIPLES, :], op=MULT)
         round_w("gpsimd", 3, None, GPSIMD_FROM, P)
         round_w("scalar", 3, 0, 0, GPSIMD_FROM)
         round_w("scalar", 3, 1, 0, GPSIMD_FROM)
@@ -189,12 +192,12 @@ def tile_picked_trilin_none_lo_kernel(tc, xT, w1, w2, w3, w4, offs, out_0, out_1
         z_bf = [sb.tile([P, HALF, PACK], BF16, name="z_bf%d" % h, align_bytes=ALIGN) for h in range(2)]
         z_codes = sb.tile([P, V], U32, name="z_codes", align_bytes=ALIGN)
         z_scales = sb.tile([P, V], U8, name="z_scales", align_bytes=ALIGN)
-        nc.vector.tensor_tensor(out=by_rows(z_bf[0][:]), in0=by_rows(y[2, 0]), in1=y12_first, op=MULT)
+        nc.vector.tensor_tensor(out=z_bf[0][:], in0=y[2, 0], in1=y12[0], op=MULT)
         spare = ps.tile([P, 3 * P], F32, name="spare", tag="bank2")
         for c0, c1 in ((0, 2 * P), (2 * P, 3 * P)):
             nc.tensor.matmul_mx(out=spare[:, c0:c1], lhsT=w_codes[2][0][:, 0:P].bitcast(FP8X4), lhsT_scale=w_scales[2][0][:, 0:P],
                                 rhs=x_codes[0][:, 0:c1 - c0].bitcast(FP8X4), rhs_scale=x_scales[0][:, 0:c1 - c0], start=True, stop=True)
-        nc.vector.tensor_tensor(out=z_bf[1][:], in0=y[2, 1], in1=y12_second[:], op=MULT)
+        nc.vector.tensor_tensor(out=z_bf[1][:], in0=y[2, 1], in1=y12[1], op=MULT)
         for u in range(2):
             quantize_half(u, z_codes, z_scales, z_bf)
             for e in range(2):

@@ -120,9 +120,9 @@ def tile_picked_trilin_none_lo_kernel(tc, xT, w1, w2, w3, w4, offs, out_0, out_1
 
         y = {}
 
-        def first_layer(d, h, tag):
+        def first_layer(d, h, tag, pairs=(1, 0)):
             target = bank("y%d_%d" % (d, h), tag, PACK)
-            for u in (1, 0):
+            for u in pairs:
                 for e in range(2):
                     one_pass(target[:, 2 * u + e, :], d, u, e, x_codes[d], x_scales[d], h)
             y[d, h] = target[:].rearrange("p t v -> p v t")
@@ -174,8 +174,8 @@ def tile_picked_trilin_none_lo_kernel(tc, xT, w1, w2, w3, w4, offs, out_0, out_1
         round_w("scalar", 2, 0, 64, SCALAR_SHARE)
         quantize_w(2, 1)
         quantize_w(2, 0)
-        for h in range(2):
-            first_layer(2, h, 2 + h)
+        first_layer(2, 0, 2)
+        first_layer(2, 1, 3, (0, 1))
 
         second = sb.tile([P, HALF, PACK], F32, name="second", tag="third_bf1", align_bytes=ALIGN)
         y12 = [w_raw[2][:, PACK - 1, :].rearrange("p (v t) -> p v t", t=PACK), second[:]]

from contextlib import ExitStack

import concourse.mybir as mybir

K, T, S, V, H = 512, 1024, 768, 256, 512
FLOPS = 2 * 4 * K * H * V

F32 = mybir.dt.float32
BF16 = mybir.dt.bfloat16
U32 = mybir.dt.uint32
I32 = mybir.dt.int32
U16 = mybir.dt.uint16
U8 = mybir.dt.uint8
FP8X4 = mybir.dt.float8_e4m3fn_x4
MULT = mybir.AluOpType.mult
ADD = mybir.AluOpType.add
COPY = mybir.ActivationFunctionType.Copy

P = 128
PACK = 4
HALF = V // 2
ALIGN = 64
SCALAR_SHARE = 96
VECTOR_TRIPLES = 64
GPSIMD_FROM = 96
EDGE = 20
MARGIN = H - 64


def tile_picked_trilin_none_lo_kernel(tc, xT, w1, w2, w3, w4, offs, out_0, out_1, out_2):
    nc = tc.nc

    def copy_on(engine, out, in_):
        if engine == "vector":
            nc.vector.tensor_copy(out=out, in_=in_)
        else:
            nc.scalar.copy(out=out, in_=in_)

    with ExitStack() as ctx:
        sb = ctx.enter_context(tc.tile_pool(name="sb", bufs=1))
        ps = ctx.enter_context(tc.psum_pool(name="ps", bufs=1))

        x_rows = xT.rearrange("(p j) c -> p j c", j=PACK)
        offsets = sb.tile([P, S // 16], U16, name="offsets")
        planes = []
        for j in range(PACK):
            plane = sb.tile([P, T], F32, name="plane%d" % j, align_bytes=ALIGN)
            nc.sync.dma_start(out=plane[:], in_=x_rows[:, j, :])
            planes.append(plane)
            if j == 0:
                nc.sync.dma_start(offsets[:], offs)
        w_raw = []
        rooms = []
        for d, w in enumerate((w1, w2, w3, w4)):
            pad = MARGIN if d == 1 else 0
            room = sb.tile([P, PACK * H + 2 * pad], F32, name="w_raw%d" % d, tag="w_raw%d" % d, align_bytes=ALIGN)
            nc.sync.dma_start(out=room[:, pad:pad + PACK * H], in_=w.rearrange("(p j) c -> p (j c)", j=PACK))
            w_raw.append(room[:, pad:pad + PACK * H].rearrange("p (j c) -> p j c", j=PACK))
            rooms.append(room)

        picked = sb.tile([P, PACK, 2 * V], BF16, name="picked", align_bytes=ALIGN)
        woven = [sb.tile([P, V, PACK], BF16, name="woven%d" % d, align_bytes=ALIGN) for d in range(3)]

        def gather_first(j):
            nc.vector.tensor_copy(out=woven[0][:, :, j], in_=planes[j][:].indirect(offsets[:, 0:V // 16]))

        def gather_rest(engine, j, c0, c1):
            looked_up = planes[j][:].indirect(offsets[:, (V + c0) // 16:(V + c1) // 16])
            if engine == "vector":
                nc.vector.tensor_copy(out=picked[:, j, c0:c1], in_=looked_up)
            else:
                nc.scalar.activation(picked[:, j, c0:c1], looked_up, COPY)

        def weave(engine, d):
            src = picked[:, :, (d - 1) * V:d * V]
            copy_on(engine, woven[d][:].rearrange("p (c i) j -> p c j i", i=4), src.rearrange("p j (c i) -> p c j i", i=4))

        x_codes = {}
        x_scales = [sb.tile([P, V], U8, name="x_scales%d" % d, align_bytes=ALIGN) for d in range(3)]

        def quantize_x(d, tag):
            x_codes[d] = sb.tile([P, V], U32, name="x_codes%d" % d, tag=tag, align_bytes=ALIGN)
            nc.vector.quantize_mx(out=x_codes[d][:].bitcast(FP8X4), scales=x_scales[d][:],
                                  in_=woven[d][:].rearrange("p c j -> p (c j)"))

        w_bf = {d: sb.tile([P, PACK, P, PACK], BF16, name="w_bf%d" % d, tag="w_bf%d" % d, align_bytes=ALIGN) for d in (0, 1, 3)}
        third_bf = [sb.tile([P, 2, P, PACK], BF16, name="third_bf%d" % u, tag="third_bf%d" % u, align_bytes=ALIGN) for u in range(2)]

        def rounded(d, u):
            if d == 2:
                return third_bf[u][:]
            return w_bf[d][:] if u is None else w_bf[d][:, 2 * u:2 * u + 2, :, :]

        w_codes = [[sb.tile([P, 2 * P], U32, name="w_codes%d_%d" % (d, u), align_bytes=ALIGN) for u in range(2)] for d in range(4)]
        w_scales = [[sb.tile([P, 2 * P], U8, name="w_scales%d_%d" % (d, u), align_bytes=ALIGN) for u in range(2)] for d in range(4)]

        def round_w(engine, d, u, m0, m1):
            tiles = slice(0, PACK) if u is None else slice(2 * u, 2 * u + 2)
            src = w_raw[d].rearrange("p j (m t) -> p m j t", t=PACK)[:, m0:m1, :, tiles]
            dst = rounded(d, u)[:, :, m0:m1, :]
            if engine == "gpsimd":
                nc.gpsimd.tensor_scalar(out=dst.rearrange("p t m j -> p m t j"), in0=src.rearrange("p m j t -> p m t j"),
                                        scalar1=1.0, scalar2=0.0, op0=MULT, op1=ADD)
            else:
                copy_on(engine, dst.rearrange("p t m j -> p m j t"), src)

        def quantize_w(d, u, e0=0, e1=2):
            cols = slice(e0 * P, e1 * P)
            nc.vector.quantize_mx(out=w_codes[d][u][:, cols].bitcast(FP8X4), scales=w_scales[d][u][:, cols],
                                  in_=rounded(d, u)[:, e0:e1, :, :].rearrange("p t m j -> p (t m j)"))

        def bank(name, tag, tiles):
            return ps.tile([P, tiles, HALF], F32, name=name, tag="bank%d" % tag)

        def one_pass(out, d, u, e, codes, scales, h):
            cols = slice(h * HALF, (h + 1) * HALF)
            m = slice(e * P, (e + 1) * P)
            nc.tensor.matmul_mx(out=out, lhsT=w_codes[d][u][:, m].bitcast(FP8X4), lhsT_scale=w_scales[d][u][:, m],
                                rhs=codes[:, cols].bitcast(FP8X4), rhs_scale=scales[:, cols], start=True, stop=True)

        y = {}

        def first_layer(d, h, tag, pairs=(1, 0)):
            target = bank("y%d_%d" % (d, h), tag, PACK)
            for u in pairs:
                for e in range(2):
                    one_pass(target[:, 2 * u + e, :], d, u, e, x_codes[d], x_scales[d], h)
            y[d, h] = target[:].rearrange("p t v -> p v t")

        def quantize_half(h, codes, scales, values):
            cols = slice(h * HALF, (h + 1) * HALF)
            nc.vector.quantize_mx(out=codes[:, cols].bitcast(FP8X4), scales=scales[:, cols],
                                  in_=values[h][:].rearrange("p v t -> p (v t)"))

        idle = sb.tile([P, 2], F32, name="idle")
        nc.gpsimd.memset(idle[:, 0:1], 0.0)
        nc.scalar.copy(out=idle[:, 1:2], in_=idle[:, 0:1])

        for j in range(PACK - 1):
            gather_first(j)
            gather_rest("scalar", j, 0, 2 * V)
        gather_rest("vector", 3, V, 2 * V)
        gather_first(3)
        gather_rest("scalar", 3, 0, V)
        quantize_x(0, "x_codes0")
        weave("scalar", 1)
        weave("vector", 2)

        round_w("scalar", 0, 0, 0, P)
        round_w("vector", 0, 1, 0, P)
        quantize_w(0, 1)
        quantize_w(0, 0)
        quantize_x(1, "w_raw0")
        for h in range(2):
            first_layer(0, h, h)

        round_w("vector", 1, 1, EDGE, P - EDGE)
        round_w("vector", 1, 0, EDGE, P - EDGE)
        round_w("scalar", 1, None, 0, EDGE)
        round_w("scalar", 1, None, P - EDGE, P)
        ends = (rooms[1][:, 0:H], rooms[1][:, PACK * H + 2 * MARGIN - H:PACK * H + 2 * MARGIN])
        y1 = [end.rearrange("p (v t) -> p v t", t=PACK) for end in ends]
        for h in range(2):
            nc.scalar.copy(out=y1[h], in_=y[0, h])
        quantize_w(1, 1)
        quantize_w(1, 0)
        quantize_x(2, "w_bf0")
        first_layer(1, 1, 0)
        first_layer(1, 0, 1)

        round_w("vector", 2, 1, 0, P)
        round_w("vector", 2, 0, SCALAR_SHARE, P)
        round_w("scalar", 2, 0, 0, 64)
        round_w("scalar", 2, 0, 64, SCALAR_SHARE)
        quantize_w(2, 1)
        quantize_w(2, 0)
        first_layer(2, 0, 2)
        first_layer(2, 1, 3, (0, 1))

        second = sb.tile([P, HALF, PACK], F32, name="second", tag="third_bf1", align_bytes=ALIGN)
        y12 = [w_raw[2][:, PACK - 1, :].rearrange("p (v t) -> p v t", t=PACK), second[:]]
        y2_part = w_raw[2][:, 0, 0:PACK * (HALF - VECTOR_TRIPLES)].rearrange("p (v t) -> p v t", t=PACK)
        nc.scalar.copy(out=y2_part, in_=y[1, 1][:, VECTOR_TRIPLES:HALF, :])
        nc.gpsimd.tensor_tensor(out=y12[1][:, VECTOR_TRIPLES:HALF, :], in0=y2_part, in1=y1[1][:, VECTOR_TRIPLES:HALF, :], op=MULT)
        nc.vector.tensor_tensor(out=y12[0], in0=y[1, 0], in1=y1[0], op=MULT)
        nc.vector.tensor_tensor(out=y12[1][:, 0:VECTOR_TRIPLES, :], in0=y[1, 1][:, 0:VECTOR_TRIPLES, :],
                                in1=y1[1][:, 0:VECTOR_TRIPLES, :], op=MULT)
        round_w("gpsimd", 3, None, GPSIMD_FROM, P)
        round_w("scalar", 3, 0, 0, GPSIMD_FROM)
        round_w("scalar", 3, 1, 0, GPSIMD_FROM)

        z_bf = [sb.tile([P, HALF, PACK], BF16, name="z_bf%d" % h, align_bytes=ALIGN) for h in range(2)]
        z_codes = sb.tile([P, V], U32, name="z_codes", align_bytes=ALIGN)
        z_scales = sb.tile([P, V], U8, name="z_scales", align_bytes=ALIGN)
        nc.vector.tensor_tensor(out=z_bf[0][:], in0=y[2, 0], in1=y12[0], op=MULT)
        spare = ps.tile([P, 3 * P], F32, name="spare", tag="bank2")
        for c0, c1 in ((0, 2 * P), (2 * P, 3 * P)):
            nc.tensor.matmul_mx(out=spare[:, c0:c1], lhsT=w_codes[2][0][:, 0:P].bitcast(FP8X4), lhsT_scale=w_scales[2][0][:, 0:P],
                                rhs=x_codes[0][:, 0:c1 - c0].bitcast(FP8X4), rhs_scale=x_scales[0][:, 0:c1 - c0], start=True, stop=True)
        nc.vector.tensor_tensor(out=z_bf[1][:], in0=y[2, 1], in1=y12[1], op=MULT)
        for u in range(2):
            quantize_half(u, z_codes, z_scales, z_bf)
            for e in range(2):
                quantize_w(3, u, e, e + 1)

        early = [bank("early%d" % h, 4 + h, 2) for h in range(2)]
        for h in range(2):
            for e in range(2):
                one_pass(early[h][:, e, :], 3, 0, e, z_codes, z_scales, h)
        last = [bank("last%d" % h, 6 + h, 2) for h in range(2)]
        for e in range(2):
            for h in (1, 0):
                one_pass(last[h][:, e, :], 3, 1, e, z_codes, z_scales, h)
        twin = bank("twin", 1, 2)
        for e in range(2):
            one_pass(twin[:, e, :], 3, 1, e, z_codes, z_scales, 0)

        r_bf = [sb.tile([P, HALF, PACK], BF16, name="r_bf%d" % h, align_bytes=ALIGN) for h in range(2)]
        r_codes = sb.tile([P, V], U32, name="r_codes", align_bytes=ALIGN)
        r_scales = sb.tile([P, V], U8, name="r_scales", align_bytes=ALIGN)
        out_rows = out_0.rearrange("(p t) v -> p t v", t=PACK)
        result = sb.tile([P, PACK, V], F32, name="result", tag="w_bf3", align_bytes=ALIGN)
        nc.scalar.copy(out=result[:, 0:2, 0:HALF], in_=early[0][:])
        nc.scalar.copy(out=r_bf[0][:, :, 0:2], in_=early[0][:].rearrange("p t v -> p v t"))
        nc.vector.tensor_copy(out=result[:, 0:2, HALF:V], in_=early[1][:])
        nc.sync.dma_start(out=out_rows[:, 0:2, :], in_=result[:, 0:2, :])
        nc.scalar.copy(out=r_bf[0][:, :, 2:4], in_=last[0][:].rearrange("p t v -> p v t"))
        nc.vector.tensor_copy(out=result[:, 2:4, HALF:V], in_=last[1][:])
        nc.vector.tensor_copy(out=result[:, 2:4, 0:HALF], in_=twin[:])
        nc.sync.dma_start(out=out_rows[:, 2:4, :], in_=result[:, 2:4, :])
        nc.vector.tensor_copy(out=r_bf[1][:].rearrange("p (c i) t -> p c t i", i=4),
                              in_=result[:, :, HALF:V].rearrange("p t (c i) -> p c t i", i=4))
        for h in range(2):
            quantize_half(h, r_codes, r_scales, r_bf)
        words = out_1.rearrange("z p c r -> (z p) (c r)").bitcast(I32)
        nc.sync.dma_start(out=words, in_=r_codes[:].bitcast(I32))
        rows = out_2.rearrange("z q c -> (z q) c").bitcast(I32)
        for q in range(4):
            queue = nc.scalar if q < 3 else nc.sync
            queue.dma_start(out=rows[4 * q:4 * q + 4, :], in_=r_scales[32 * q:32 * q + 4, :].bitcast(I32))
